import numpy as np
import ml_dtypes


def mxq(x, axis, fmt="e4m3"):
    dtype, down = {"e4m3": (ml_dtypes.float8_e4m3fn, 7), "e5m2": (ml_dtypes.float8_e5m2, 14)}[fmt]
    v = np.moveaxis(np.asarray(x, np.float32).astype(ml_dtypes.bfloat16).astype(np.float64), axis, -1)
    blocks = v.reshape(v.shape[:-1] + (-1, 32))
    amax = np.abs(blocks).max(-1, keepdims=True)
    byte = np.maximum(np.where(amax > 0, np.frexp(amax)[1] - 1 + 127, 0) - down, 1)
    scale = np.exp2(byte - 127.0)
    codes = (blocks / scale).astype(np.float32).astype(dtype).astype(np.float64)
    return np.moveaxis((codes * scale).reshape(v.shape), -1, axis)


WIDE = False


def mx_kscale(k):
    if not WIDE:
        return np.ones(k)
    levels = np.array([10, -10, 5, -5, 0])
    if k % 512:
        return np.exp2(np.random.permutation(np.resize(levels, k // 32))).repeat(32)
    a = np.empty((k // 512, 16))
    for p in range(k // 512):
        a[p, :8] = np.random.permutation(np.resize(levels, 8))
        for g in range(8):
            far = levels[np.abs(levels - a[p, g]) >= 10]
            a[p, g + 8] = far[np.random.randint(len(far))]
    return np.exp2(a.ravel()).repeat(32)


BF16 = ml_dtypes.bfloat16


def bf(x):
    return np.asarray(x, np.float32).astype(BF16)


def f64(x):
    return np.asarray(x).astype(np.float64)


E2M1 = np.array([0.0, 0.5, 1.0, 1.5, 2.0, 3.0, 4.0, 6.0, -0.0, -0.5, -1.0, -1.5, -2.0, -3.0, -4.0, -6.0])


def pack_weight(w, fmt):
    k, n = w.shape
    w = f64(bf(w)).reshape(k // 32, 32, n)
    amax = np.abs(w).max(1)
    if fmt == "e4m3":
        byte = np.frexp(amax)[1] - 1 + 127 - 7
    else:
        mant, ex = np.frexp(amax / 6.0)
        byte = np.where(mant > 0.5, ex, ex - 1) + 127
    byte = np.clip(np.where(amax > 0, byte, 1), 1, 254)
    scaled = (w * np.exp2(127.0 - byte)[:, None, :]).reshape(k, n).astype(np.float32)
    by_word = np.ascontiguousarray(scaled.reshape(k // 512, 128, 4, n).transpose(0, 1, 3, 2))
    if fmt == "e4m3":
        words = by_word.astype(ml_dtypes.float8_e4m3fn).view(np.uint8)
    else:
        c = by_word.astype(ml_dtypes.float4_e2m1fn).view(np.uint8) & 0xF
        words = c[..., 0::2] | (c[..., 1::2] << 4)
    return np.ascontiguousarray(words), np.ascontiguousarray(byte.astype(np.uint8).reshape(k // 512, 16, n))


def unpack_weight(words, scales, fmt):
    g, p, n, _ = words.shape
    if fmt == "e4m3":
        vals = np.ascontiguousarray(words).view(ml_dtypes.float8_e4m3fn).astype(np.float64)
    else:
        nib = np.empty((g, p, n, 4), np.uint8)
        nib[..., 0::2] = words & 0xF
        nib[..., 1::2] = words >> 4
        vals = E2M1[nib]
    vals = vals * np.repeat(np.exp2(scales.astype(np.float64) - 127.0), 8, axis=1)[..., None]
    return vals.transpose(0, 1, 3, 2).reshape(g * 512, n)


N, P, Q, M, A = 1024, 512, 1024, 1024, 2


def sigmoid(z):
    return 1.0 / (1.0 + np.exp(-z))


def aipw_score(mu0, mu1, p, t, y):
    return mu1 - mu0 + t * (y - mu1) / p - (1.0 - t) * (y - mu0) / (1.0 - p)


def draw0():
    s, u = mx_kscale(P), mx_kscale(N)
    x = np.random.standard_normal((N, P)) * s
    b = np.random.standard_normal((A, P, Q)) / np.sqrt(P) / s[None, :, None]
    gam = np.random.standard_normal((P, Q)) / np.sqrt(P) / s[:, None]
    gam_words, gam_scales = pack_weight(gam, "e4m3")
    lat = np.random.standard_normal((N, Q))
    y = np.random.standard_normal((N, Q))
    v = np.random.standard_normal((N, M)) / u[:, None]
    w = (1.0 + 0.1 * np.random.standard_normal(N)) * u
    return {"x": bf(x), "b": bf(b), "gam_words": gam_words, "gam_scales": gam_scales, "lat": bf(lat), "y": bf(y), "v": bf(v), "w": bf(w)}


def core(x, b, gam_words, gam_scales, lat, y, v, w):
    xq = mxq(f64(x), 1, "e4m3")
    bb = f64(b)
    mu0 = xq @ mxq(bb[0], 0, "e4m3")
    mu1 = xq @ mxq(bb[1], 0, "e4m3")
    raw = sigmoid(xq @ unpack_weight(gam_words, gam_scales, "e4m3"))
    p = np.minimum(np.maximum(raw, 0.15), 0.85)
    t = np.where(f64(lat) > 0.0, 1.0, 0.0)
    psi = aipw_score(mu0, mu1, p, t, f64(y))
    g = f64(w)[:, None] * psi
    root_n = np.sqrt(x.shape[0])
    return (mxq(f64(v), 0, "e4m3").T @ mxq(g, 0, "e4m3")) / root_n


def e4m3fn_bytes(y):
    return np.clip(np.asarray(y, np.float64), -448.0, 448.0).astype(np.float32).astype(ml_dtypes.float8_e4m3fn).view(np.uint8)


def e4m3fn_values(b):
    return np.asarray(b, np.uint8).view(ml_dtypes.float8_e4m3fn).astype(np.float64)


def setup_inputs():
    d = draw0()
    x0 = np.asarray(d['v']).astype(np.float64)
    s = (np.max(np.abs(x0), axis=(1,), keepdims=True) / 448.0).astype(np.float32)
    out = {}
    for k, v in d.items():
        if k == 'v':
            out['v_bytes'] = e4m3fn_bytes(x0 / s.astype(np.float64))
            out['v_scale'] = s
        else:
            out[k] = v
    return out


def reference(x, b, gam_words, gam_scales, lat, y, v_bytes, v_scale, w):
    return core(x, b, gam_words, gam_scales, lat, y, e4m3fn_values(v_bytes) * v_scale.astype(np.float64), w)

@@ -1,0 +1,434 @@
+import math
+from contextlib import ExitStack
+
+import concourse.mybir as mybir
+from concourse.masks import make_identity
+
+N, KX, Q, M = 1024, 512, 1024, 1024
+FLOPS = 2 * N * KX * Q * 3 + 2 * N * M * Q
+
+F32 = mybir.dt.float32
+BF16 = mybir.dt.bfloat16
+I32 = mybir.dt.int32
+U32 = mybir.dt.uint32
+U8 = mybir.dt.uint8
+FP8 = mybir.dt.float8_e4m3fn
+FP8X4 = mybir.dt.float8_e4m3fn_x4
+ALU = mybir.AluOpType
+ACT = mybir.ActivationFunctionType
+
+P = 128
+PACK = 4
+BANK = 512
+PART = 256
+GROUPS = N // (P * PACK)
+PARTS = Q // PART
+CHUNKS = [256, 256, 256, 128, 128]
+TRIM = 0.15
+ODDS_LO = TRIM / (1.0 - TRIM)
+ODDS_HI = (1.0 - TRIM) / TRIM
+RUN = 4
+
+
+def tile_aipwscorebasismoments_w8_kernel(tc, x, b, gam_words, gam_scales, lat, y, v_bytes, v_scale, w, out):
+    nc = tc.nc
+    with ExitStack() as ctx:
+        sb = ctx.enter_context(tc.tile_pool(name="sb", bufs=1))
+        ps = ctx.enter_context(tc.psum_pool(name="ps", bufs=1))
+        ctx.enter_context(tc.manual_schedule())
+
+        def tiles(pool, label, count, shape, dtype):
+            return [pool.tile(shape, dtype, name="%s%d" % (label, i), align_bytes=64) for i in range(count)]
+
+        def banks(label, count):
+            return [ps.tile([P, BANK], F32, name="%s%d" % (label, i)) for i in range(count)]
+
+        ident = sb.tile([P, P], F32, name="ident")
+        ln_trim = sb.tile([P, 1], F32, name="ln_trim")
+        warm = sb.tile([P, 1], F32, name="warm")
+        w_raw = sb.tile([P, GROUPS, PACK], BF16, name="w_raw")
+        w_neg = sb.tile([P, GROUPS * PACK], F32, name="w_neg")
+        v_sc = sb.tile([P, GROUPS, PACK], F32, name="v_sc")
+        x_raw = tiles(sb, "x_raw", 4, [P, 2, KX], BF16)
+        x_il = tiles(sb, "x_il", 2, [P, 2 * P * PACK], BF16)
+        x_c = tiles(sb, "x_c", 4, [P, 2 * P], U32)
+        x_s = tiles(sb, "x_s", 4, [P, 2 * P], U8)
+        b_raw = tiles(sb, "b_raw", 2 * PARTS, [P, PACK, PART], BF16)
+        b_c = tiles(sb, "b_c", 2 * PARTS, [P, PART], U32)
+        b_s = tiles(sb, "b_s", 2 * PARTS, [P, PART], U8)
+        il = tiles(sb, "il", 4, [P, PART * PACK], BF16)
+        gam_first = sb.tile([P, PART], U32, name="gam_first", align_bytes=64)
+        gam_rest = sb.tile([P, Q - PART], U32, name="gam_rest", align_bytes=64)
+        gam_s = sb.tile([P, Q], U8, name="gam_s", align_bytes=64)
+        lat_first = tiles(sb, "lat_first", GROUPS, [P, PACK, PART], BF16)
+        lat_rest = tiles(sb, "lat_rest", GROUPS, [P, PACK, Q - PART], BF16)
+        y_first = tiles(sb, "y_first", GROUPS, [P, PACK, PART], BF16)
+        y_rest = tiles(sb, "y_rest", GROUPS, [P, PACK, Q - PART], BF16)
+        v_raw = tiles(sb, "v_raw", GROUPS, [P, PACK, M], U8)
+        v_wide = tiles(sb, "v_wide", GROUPS, [P, PACK, M], BF16)
+        v_c = tiles(sb, "v_c", GROUPS, [P, M], U32)
+        v_s = tiles(sb, "v_s", GROUPS, [P, M], U8)
+        g_rows = tiles(sb, "g_rows", 2, [P, PACK, PART], BF16)
+        g_il = tiles(sb, "g_il", 2, [P, PART * PACK], BF16)
+        g_c = tiles(sb, "g_c", GROUPS, [P, Q], U32)
+        g_s = tiles(sb, "g_s", GROUPS, [P, Q], U8)
+        f_t = tiles(sb, "f_t", 4, [P, BANK], F32)
+        e_t = tiles(sb, "e_t", 4, [P, BANK], F32)
+        n_t = tiles(sb, "n_t", 3, [P, BANK], F32)
+        a_t = tiles(sb, "a_t", 3, [P, BANK], F32)
+        o_t = tiles(sb, "o_t", 8, [P, BANK], F32)
+        z_ps = banks("z_ps", 2)
+        mu_ps = banks("mu_ps", 2)
+        d_ps = banks("d_ps", 2)
+        o_ps = banks("o_ps", 2)
+
+        units = []
+        col = 0
+        for width in CHUNKS:
+            count = BANK // width
+            for g in range(GROUPS):
+                for t0 in range(0, PACK, count):
+                    units.append((col, width, g, t0, count))
+            col = col + width
+        last = len(units) - 1
+
+        x_rows = x.rearrange("(g p t) k -> g p t k", p=P, t=PACK)
+        lat_rows = lat.rearrange("(g p t) q -> g p t q", p=P, t=PACK)
+        y_rows = y.rearrange("(g p t) q -> g p t q", p=P, t=PACK)
+        v_rows = v_bytes.rearrange("(g p t) m -> g p t m", p=P, t=PACK)
+        gam_flat = gam_words[0].rearrange("p n t -> p (n t)")
+
+        def load_x(j):
+            nc.sync.dma_start(out=x_raw[j][:], in_=x_rows[j // 2][:, 2 * (j % 2) : 2 * (j % 2) + 2, :])
+
+        def load_b(arm, part):
+            rows = b[arm].rearrange("(p j) q -> p j q", j=PACK)
+            nc.sync.dma_start(out=b_raw[arm * PARTS + part][:], in_=rows[:, :, part * PART : (part + 1) * PART])
+
+        nc.vector.memset(gam_s[:].bitcast(I32), 0)
+        nc.vector.memset(warm[:], 1.0)
+        nc.vector.tensor_scalar(out=ln_trim[:], in0=warm[:], scalar1=math.log(TRIM), scalar2=None, op0=ALU.mult)
+        make_identity(nc, ident[:])
+        load_x(0)
+        load_b(1, 0)
+        for quad in range(4):
+            nc.scalar.dma_start(
+                out=gam_s[32 * quad : 32 * quad + 4, :].bitcast(I32),
+                in_=gam_scales[0, 4 * quad : 4 * quad + 4, :].bitcast(I32),
+            )
+        nc.scalar.activation(out=warm[:], in_=ln_trim[:], func=ACT.Exp)
+        nc.sync.dma_start(out=gam_first[:].bitcast(I32), in_=gam_flat[:, : PART * PACK].bitcast(I32))
+        load_x(1)
+        load_b(0, 0)
+        nc.sync.dma_start(out=y_first[0][:], in_=y_rows[0][:, :, :PART])
+        nc.sync.dma_start(out=lat_first[0][:], in_=lat_rows[0][:, :, :PART])
+        nc.sync.dma_start(out=w_raw[:], in_=w.rearrange("(g p t) -> p g t", p=P, t=PACK))
+        load_x(2)
+        load_x(3)
+        nc.sync.dma_start(out=lat_first[1][:], in_=lat_rows[1][:, :, :PART])
+        nc.sync.dma_start(out=y_first[1][:], in_=y_rows[1][:, :, :PART])
+        load_b(1, 1)
+        load_b(0, 1)
+        nc.sync.dma_start(out=v_sc[:], in_=v_scale.rearrange("(g p t) o -> p g (t o)", p=P, t=PACK))
+        nc.sync.dma_start(out=v_raw[0][:], in_=v_rows[0])
+        nc.sync.dma_start(out=gam_rest[:].bitcast(I32), in_=gam_flat[:, PART * PACK :].bitcast(I32))
+        nc.sync.dma_start(out=v_raw[1][:], in_=v_rows[1])
+        nc.sync.dma_start(out=lat_rest[0][:], in_=lat_rows[0][:, :, PART:])
+        nc.sync.dma_start(out=y_rest[0][:], in_=y_rows[0][:, :, PART:])
+        load_b(1, 2)
+        load_b(0, 2)
+        nc.sync.dma_start(out=lat_rest[1][:], in_=lat_rows[1][:, :, PART:])
+        nc.sync.dma_start(out=y_rest[1][:], in_=y_rows[1][:, :, PART:])
+        load_b(1, 3)
+        load_b(0, 3)
+
+        def quantize(codes, scales, src):
+            nc.vector.quantize_mx(out=codes.bitcast(FP8X4), scales=scales, in_=src)
+
+        def interleave(on_vector, dst, src, scale):
+            dst_v = dst.rearrange("p (c i t) -> p c t i", i=RUN, t=PACK)
+            src_v = src.rearrange("p t (c i) -> p c t i", i=RUN)
+            if on_vector and scale == 1.0:
+                nc.vector.tensor_copy(out=dst_v, in_=src_v)
+            elif on_vector:
+                nc.vector.tensor_scalar(out=dst_v, in0=src_v, scalar1=scale, scalar2=None, op0=ALU.mult)
+            elif scale == 1.0:
+                nc.scalar.copy(out=dst_v, in_=src_v)
+            else:
+                nc.scalar.activation(out=dst_v, in_=src_v, func=ACT.Copy, scale=scale)
+
+        def x_turn(j):
+            words = x_raw[j][:].rearrange("p a k -> p (a k)").bitcast(F32)
+            bank = o_ps[j % 2]
+            half = KX // 2
+            for a in range(2):
+                for u in range(2):
+                    nc.tensor.transpose(bank[:, (2 * a + u) * P : (2 * a + u + 1) * P], words[:, a * half + u : (a + 1) * half : 2], ident[:])
+
+        def x_copy(j):
+            nc.scalar.copy(
+                out=x_il[j % 2][:].bitcast(F32).rearrange("p (a r u) -> p a r u", a=2, u=2),
+                in_=o_ps[j % 2][:].rearrange("p (a u r) -> p a r u", a=2, u=2),
+            )
+
+        def x_quant(j):
+            quantize(x_c[j][:], x_s[j][:], x_il[j % 2][:])
+
+        def x_operand(g, t):
+            j = 2 * g + t // 2
+            cols = slice((t % 2) * P, (t % 2 + 1) * P)
+            return x_c[j][:, cols].bitcast(FP8X4), x_s[j][:, cols]
+
+        def b_operand(arm, col0, width):
+            k = arm * PARTS + col0 // PART
+            cols = slice(col0 % PART, col0 % PART + width)
+            return b_c[k][:, cols].bitcast(FP8X4), b_s[k][:, cols]
+
+        def gam_operand(col0, width):
+            if col0 < PART:
+                codes = gam_first[:, col0 : col0 + width]
+            else:
+                codes = gam_rest[:, col0 - PART : col0 - PART + width]
+            return codes.bitcast(FP8X4), gam_s[:, col0 : col0 + width]
+
+        def stage1(bank, s, movers):
+            col0, width, g, t0, count = units[s]
+            for i in range(count):
+                lhs, lhs_s = x_operand(g, t0 + i)
+                for n, (rhs, rhs_s) in enumerate(movers):
+                    nc.tensor.matmul_mx(out=bank[:, i * width : (i + 1) * width], lhsT=lhs, lhsT_scale=lhs_s, rhs=rhs, rhs_scale=rhs_s,
+                                        start=(n == 0), stop=(n == len(movers) - 1))
+
+        def mm_z(s):
+            stage1(z_ps[s % 2], s, [gam_operand(units[s][0], units[s][1])])
+
+        def mm_mu(s):
+            stage1(mu_ps[s % 2], s, [b_operand(1, units[s][0], units[s][1])])
+
+        def mm_d(s):
+            stage1(d_ps[s % 2], s, [b_operand(1, units[s][0], units[s][1]), b_operand(0, units[s][0], units[s][1])])
+
+        def rows_of(first, rest, s):
+            col0, width, g, t0, count = units[s]
+            if col0 < PART:
+                return first[g][:, t0 : t0 + count, col0 : col0 + width]
+            return rest[g][:, t0 : t0 + count, col0 - PART : col0 - PART + width]
+
+        def by_t(tile_ap, s):
+            return tile_ap.rearrange("p (t c) -> p t c", t=units[s][4])
+
+        def exps(s):
+            nc.scalar.activation(out=f_t[s % 4][:], in_=z_ps[s % 2][:], func=ACT.Exp, scale=-1.0)
+            nc.scalar.activation(out=e_t[s % 4][:], in_=z_ps[s % 2][:], func=ACT.Exp, bias=ln_trim[:])
+
+        def op_mask(s):
+            nc.vector.tensor_scalar(out=by_t(n_t[s % 3][:], s), in0=rows_of(lat_first, lat_rest, s), scalar1=0.0, scalar2=TRIM,
+                                    op0=ALU.is_le, op1=ALU.subtract)
+
+        def op_clip(s):
+            nc.vector.tensor_scalar(out=f_t[s % 4][:], in0=f_t[s % 4][:], scalar1=ODDS_LO, scalar2=ODDS_HI, op0=ALU.max, op1=ALU.min)
+
+        def op_resid(s):
+            nc.vector.tensor_tensor(out=by_t(a_t[s % 3][:], s), in0=rows_of(y_first, y_rest, s), in1=by_t(mu_ps[s % 2][:], s), op=ALU.subtract)
+
+        def op_weigh(s):
+            nc.vector.scalar_tensor_tensor(out=a_t[s % 3][:], in0=f_t[s % 4][:], scalar=1.0, in1=a_t[s % 3][:], op0=ALU.add, op1=ALU.mult)
+
+        def op_contrast(s):
+            nc.vector.tensor_tensor(out=a_t[s % 3][:], in0=a_t[s % 3][:], in1=d_ps[s % 2][:], op=ALU.add)
+
+        def op_arm(s):
+            nc.vector.scalar_tensor_tensor(out=e_t[s % 4][:], in0=e_t[s % 4][:], scalar=TRIM * ODDS_LO, in1=n_t[s % 3][:], op0=ALU.max, op1=ALU.min)
+
+        def block_of(s):
+            return len([1 for r in range(s) if units[r][3] + units[r][4] == PACK])
+
+        def op_score(s):
+            col0, width, g, t0, count = units[s]
+            for i in range(count):
+                t = t0 + i
+                cols = slice(i * width, (i + 1) * width)
+                nc.vector.scalar_tensor_tensor(out=g_rows[block_of(s) % 2][:, t, :width], in0=a_t[s % 3][:, cols],
+                                               scalar=w_neg[:, g * PACK + t : g * PACK + t + 1], in1=e_t[s % 4][:, cols],
+                                               op0=ALU.mult, op1=ALU.mult)
+
+        def closes_block(s):
+            return units[s][3] + units[s][4] == PACK
+
+        def g_weave(s, on_vector):
+            width = units[s][1]
+            interleave(on_vector, g_il[block_of(s) % 2][:, : width * PACK], g_rows[block_of(s) % 2][:, :, :width], 1.0)
+
+        def g_quant(s):
+            col0, width, g, t0, count = units[s]
+            quantize(g_c[g][:, col0 : col0 + width], g_s[g][:, col0 : col0 + width], g_il[block_of(s) % 2][:, : width * PACK])
+
+        slot = []
+
+        def b_weave(arm, part, on_vector):
+            buf = il[len(slot) % 4]
+            slot.append(1)
+            interleave(on_vector, buf[:], b_raw[arm * PARTS + part][:], 1.0 if arm == 1 else -1.0)
+            return lambda: quantize(b_c[arm * PARTS + part][:], b_s[arm * PARTS + part][:], buf[:])
+
+        def v_widen(g, t, on_vector):
+            if on_vector:
+                nc.vector.tensor_scalar(out=v_wide[g][:, t, :], in0=v_raw[g][:, t, :].bitcast(FP8), scalar1=v_sc[:, g, t : t + 1], scalar2=None, op0=ALU.mult)
+            else:
+                nc.scalar.activation(out=v_wide[g][:, t, :], in_=v_raw[g][:, t, :].bitcast(FP8), func=ACT.Copy, scale=v_sc[:, g, t : t + 1])
+
+        def v_weave(g, part, on_vector):
+            buf = il[len(slot) % 4]
+            slot.append(1)
+            cols = slice(part * PART, (part + 1) * PART)
+            interleave(on_vector, buf[:], v_wide[g][:, :, cols], 1.0)
+            return lambda: quantize(v_c[g][:, cols], v_s[g][:, cols], buf[:])
+
+        outs = []
+        col = 0
+        for width in CHUNKS:
+            for j0 in range(0, M // P, BANK // width):
+                outs.append((col, width, j0))
+            col = col + width
+
+        def mm_out(k):
+            col0, width, j0 = outs[k]
+            for i in range(BANK // width):
+                m_cols = slice((j0 + i) * P, (j0 + i + 1) * P)
+                for g in range(GROUPS):
+                    nc.tensor.matmul_mx(out=o_ps[k % 2][:, i * width : (i + 1) * width], lhsT=v_c[g][:, m_cols].bitcast(FP8X4), lhsT_scale=v_s[g][:, m_cols],
+                                        rhs=g_c[g][:, col0 : col0 + width].bitcast(FP8X4), rhs_scale=g_s[g][:, col0 : col0 + width],
+                                        start=(g == 0), stop=(g == GROUPS - 1))
+
+        def copy_out(k, on_vector, queue):
+            col0, width, j0 = outs[k]
+            count = BANK // width
+            if on_vector:
+                nc.vector.tensor_scalar(out=o_t[k % 8][:], in0=o_ps[k % 2][:], scalar1=1.0 / math.sqrt(N), scalar2=None, op0=ALU.mult)
+            else:
+                nc.scalar.activation(out=o_t[k % 8][:], in_=o_ps[k % 2][:], func=ACT.Copy, scale=1.0 / math.sqrt(N))
+            dst = out[j0 * P : (j0 + count) * P, col0 : col0 + width].rearrange("(j p) q -> p j q", p=P)
+            queue.dma_start(out=dst, in_=o_t[k % 8][:].rearrange("p (j q) -> p j q", j=count))
+
+        x_turn(0)
+        x_copy(0)
+        x_turn(1)
+        quant_b1 = b_weave(1, 0, True)
+        x_quant(0)
+        quant_b1()
+        mm_z(0)
+        mm_mu(0)
+        x_copy(1)
+        exps(0)
+        quant_b0 = b_weave(0, 0, True)
+        x_quant(1)
+        quant_b0()
+        mm_z(1)
+        mm_d(0)
+        mm_mu(1)
+        x_turn(2)
+        x_turn(3)
+        exps(1)
+        x_copy(2)
+        x_copy(3)
+        op_resid(0)
+        op_mask(0)
+        op_clip(0)
+        nc.vector.tensor_scalar(out=w_neg[:], in0=w_raw[:].rearrange("p g t -> p (g t)"), scalar1=-1.0 / TRIM, scalar2=None, op0=ALU.mult)
+        op_arm(0)
+        op_mask(1)
+        x_quant(2)
+        x_quant(3)
+        mm_z(2)
+
+        SIDE = [
+            [("b", 1, 1, False), ("b", 0, 1, False)],
+            [("vw", 0, 0, False), ("vw", 0, 1, False), ("vw", 0, 2, False)],
+            [("vw", 0, 3, False), ("vw", 1, 0, False)],
+            [("vw", 1, 1, False), ("vw", 1, 2, False), ("vw", 1, 3, False)],
+            [("b", 1, 2, False)],
+            [("b", 0, 2, False), ("vi", 0, 0, False)],
+            [("vi", 1, 0, False)],
+            [("vi", 0, 1, False), ("vi", 1, 1, False)],
+            [("b", 1, 3, False)],
+            [("b", 0, 3, False), ("vi", 0, 2, False)],
+            [("vi", 1, 2, False)],
+            [("vi", 0, 3, False), ("vi", 1, 3, False)],
+            [("o", 3, False)] * 3,
+            [("o", 12, False)] * 4,
+            [("o", 12, False)] * 5,
+            [("o", 14, False)] * 2,
+        ]
+
+        pending = []
+        made = 0
+        copied = 0
+        for s in range(len(units)):
+            if s + 3 <= last:
+                pass_z = s + 3
+            else:
+                pass_z = None
+            if s + 2 <= last:
+                exps(s + 2)
+            if pass_z is not None:
+                mm_z(pass_z)
+            if s + 2 <= last:
+                mm_mu(s + 2)
+            if s + 1 <= last:
+                mm_d(s + 1)
+            quants = pending
+            pending = []
+            on_dve = []
+            if s >= 1 and closes_block(s - 1):
+                g_weave(s - 1, False)
+                quants.append(lambda r=s - 1: g_quant(r))
+            for job in SIDE[s]:
+                if job[-1]:
+                    on_dve.append(job)
+                elif job[0] == "b":
+                    pending.append(b_weave(job[1], job[2], False))
+                elif job[0] == "vw":
+                    v_widen(job[1], job[2], False)
+                elif job[0] == "vi":
+                    pending.append(v_weave(job[1], job[2], False))
+                else:
+                    while made < min(copied + 2, job[1]):
+                        mm_out(made)
+                        made = made + 1
+                    copy_out(copied, False, nc.sync)
+                    copied = copied + 1
+                    if made < job[1]:
+                        mm_out(made)
+                        made = made + 1
+            if s + 1 <= last:
+                op_clip(s + 1)
+            op_weigh(s)
+            if s + 1 <= last:
+                op_resid(s + 1)
+            op_contrast(s)
+            if s + 1 <= last:
+                op_arm(s + 1)
+            op_score(s)
+            if s + 2 <= last:
+                op_mask(s + 2)
+            for job in on_dve:
+                if job[0] == "vw":
+                    v_widen(job[1], job[2], True)
+                elif job[0] == "vi":
+                    pending.append(v_weave(job[1], job[2], True))
+                else:
+                    pending.append(b_weave(job[1], job[2], True))
+            for run in quants:
+                run()
+
+        for run in pending:
+            run()
+        g_weave(last, True)
+        g_quant(last)
+        while copied < len(outs):
+            while made < min(copied + 2, len(outs)):
+                mm_out(made)
+                made = made + 1
+            at_end = copied == len(outs) - 1
+            copy_out(copied, at_end, nc.sync if (at_end or copied < len(outs) - 2) else nc.scalar)
+            copied = copied + 1

@@ -20,14 +20,20 @@ ACT = mybir.ActivationFunctionType
 P = 128
 PACK = 4
 BANK = 512
-PART = 256
 GROUPS = N // (P * PACK)
+PAIRS = GROUPS * PACK // 2
+PART = 256
 PARTS = Q // PART
 CHUNKS = [256, 256, 256, 128, 128]
 TRIM = 0.15
 ODDS_LO = TRIM / (1.0 - TRIM)
 ODDS_HI = (1.0 - TRIM) / TRIM
 RUN = 4
+SCALAR_ROOM = 6
+EXP_DEPTH = 4
+MID_DEPTH = 3
+WEAVE_DEPTH = 6
+STAGE_DEPTH = 8
 
 
 def tile_aipwscorebasismoments_w8_kernel(tc, x, b, gam_words, gam_scales, lat, y, v_bytes, v_scale, w, out):
@@ -37,59 +43,62 @@ def tile_aipwscorebasismoments_w8_kernel(tc, x, b, gam_words, gam_scales, lat, y
         ps = ctx.enter_context(tc.psum_pool(name="ps", bufs=1))
         ctx.enter_context(tc.manual_schedule())
 
-        def tiles(pool, label, count, shape, dtype):
-            return [pool.tile(shape, dtype, name="%s%d" % (label, i), align_bytes=64) for i in range(count)]
+        def tiles(label, count, shape, dtype):
+            return [sb.tile(shape, dtype, name="%s%d" % (label, i), align_bytes=64) for i in range(count)]
 
         def banks(label, count):
             return [ps.tile([P, BANK], F32, name="%s%d" % (label, i)) for i in range(count)]
 
         ident = sb.tile([P, P], F32, name="ident")
+        ident_bf = sb.tile([P, P], BF16, name="ident_bf")
         ln_trim = sb.tile([P, 1], F32, name="ln_trim")
-        warm = sb.tile([P, 1], F32, name="warm")
+        zero = sb.tile([P, 1], F32, name="zero")
+        one = sb.tile([P, 1], F32, name="one")
         w_raw = sb.tile([P, GROUPS, PACK], BF16, name="w_raw")
-        w_neg = sb.tile([P, GROUPS * PACK], F32, name="w_neg")
-        v_sc = sb.tile([P, GROUPS, PACK], F32, name="v_sc")
-        x_raw = tiles(sb, "x_raw", 4, [P, 2, KX], BF16)
-        x_il = tiles(sb, "x_il", 2, [P, 2 * P * PACK], BF16)
-        x_c = tiles(sb, "x_c", 4, [P, 2 * P], U32)
-        x_s = tiles(sb, "x_s", 4, [P, 2 * P], U8)
-        b_raw = tiles(sb, "b_raw", 2 * PARTS, [P, PACK, PART], BF16)
-        b_c = tiles(sb, "b_c", 2 * PARTS, [P, PART], U32)
-        b_s = tiles(sb, "b_s", 2 * PARTS, [P, PART], U8)
-        il = tiles(sb, "il", 4, [P, PART * PACK], BF16)
+        w_fac = sb.tile([P, GROUPS * PACK], F32, name="w_fac")
+        v_fac = sb.tile([P, GROUPS, PACK], F32, name="v_fac")
+        x_raw = tiles("x_raw", PAIRS, [P, 2, KX], BF16)
+        x_woven = tiles("x_woven", 2, [P, 2 * P * PACK], BF16)
+        x_codes = tiles("x_codes", PAIRS, [P, 2 * P], U32)
+        x_scales = tiles("x_scales", PAIRS, [P, 2 * P], U8)
+        b_raw = tiles("b_raw", 2 * PARTS, [P, PACK, PART], BF16)
+        b_codes = tiles("b_codes", 2 * PARTS, [P, PART], U32)
+        b_scales = tiles("b_scales", 2 * PARTS, [P, PART], U8)
+        woven = tiles("woven", WEAVE_DEPTH, [P, PART * PACK], BF16)
         gam_first = sb.tile([P, PART], U32, name="gam_first", align_bytes=64)
         gam_rest = sb.tile([P, Q - PART], U32, name="gam_rest", align_bytes=64)
-        gam_s = sb.tile([P, Q], U8, name="gam_s", align_bytes=64)
-        lat_first = tiles(sb, "lat_first", GROUPS, [P, PACK, PART], BF16)
-        lat_rest = tiles(sb, "lat_rest", GROUPS, [P, PACK, Q - PART], BF16)
-        y_first = tiles(sb, "y_first", GROUPS, [P, PACK, PART], BF16)
-        y_rest = tiles(sb, "y_rest", GROUPS, [P, PACK, Q - PART], BF16)
-        v_raw = tiles(sb, "v_raw", GROUPS, [P, PACK, M], U8)
-        v_wide = tiles(sb, "v_wide", GROUPS, [P, PACK, M], BF16)
-        v_c = tiles(sb, "v_c", GROUPS, [P, M], U32)
-        v_s = tiles(sb, "v_s", GROUPS, [P, M], U8)
-        g_rows = tiles(sb, "g_rows", 2, [P, PACK, PART], BF16)
-        g_il = tiles(sb, "g_il", 2, [P, PART * PACK], BF16)
-        g_c = tiles(sb, "g_c", GROUPS, [P, Q], U32)
-        g_s = tiles(sb, "g_s", GROUPS, [P, Q], U8)
-        f_t = tiles(sb, "f_t", 4, [P, BANK], F32)
-        e_t = tiles(sb, "e_t", 4, [P, BANK], F32)
-        n_t = tiles(sb, "n_t", 3, [P, BANK], F32)
-        a_t = tiles(sb, "a_t", 3, [P, BANK], F32)
-        o_t = tiles(sb, "o_t", 8, [P, BANK], F32)
+        gam_plane = sb.tile([P, Q], U8, name="gam_plane", align_bytes=64)
+        lat_first = tiles("lat_first", PAIRS, [P, 2, PART], BF16)
+        lat_rest = tiles("lat_rest", GROUPS, [P, PACK, Q - PART], BF16)
+        y_first = tiles("y_first", PAIRS, [P, 2, PART], BF16)
+        y_rest = tiles("y_rest", GROUPS, [P, PACK, Q - PART], BF16)
+        v_raw = tiles("v_raw", PAIRS, [P, 2, M], U8)
+        v_wide = tiles("v_wide", GROUPS, [P, PACK, M], BF16)
+        v_codes = tiles("v_codes", GROUPS, [P, M], U32)
+        v_scales = tiles("v_scales", GROUPS, [P, M], U8)
+        g_rows = tiles("g_rows", 2, [P, PACK, PART], BF16)
+        g_woven = tiles("g_woven", 2, [P, PART * PACK], BF16)
+        g_codes = tiles("g_codes", GROUPS, [P, Q], U32)
+        g_scales = tiles("g_scales", GROUPS, [P, Q], U8)
+        exp_neg = tiles("exp_neg", EXP_DEPTH, [P, BANK], F32)
+        exp_pos = tiles("exp_pos", EXP_DEPTH, [P, BANK], F32)
+        cap = tiles("cap", MID_DEPTH, [P, BANK], F32)
+        acc = tiles("acc", MID_DEPTH, [P, BANK], F32)
+        stage = tiles("stage", STAGE_DEPTH, [P, BANK], F32)
         z_ps = banks("z_ps", 2)
-        mu_ps = banks("mu_ps", 2)
-        d_ps = banks("d_ps", 2)
-        o_ps = banks("o_ps", 2)
+        mu_ps = ps.tile([P, BANK], F32, name="mu_ps")
+        resid_ps = banks("resid_ps", 2)
+        diff_ps = ps.tile([P, BANK], F32, name="diff_ps")
+        mu_neg = tiles("mu_neg", 2, [P, BANK], F32)
+        out_ps = banks("out_ps", 2)
 
         units = []
-        col = 0
-        for width in CHUNKS:
+        outs = []
+        for c, width in enumerate(CHUNKS):
+            col0 = sum(CHUNKS[:c])
             count = BANK // width
-            for g in range(GROUPS):
-                for t0 in range(0, PACK, count):
-                    units.append((col, width, g, t0, count))
-            col = col + width
+            units.extend((col0, width, g, t0, count) for g in range(GROUPS) for t0 in range(0, PACK, count))
+            outs.extend((col0, width, j0) for j0 in range(0, M // P, count))
         last = len(units) - 1
 
         x_rows = x.rearrange("(g p t) k -> g p t k", p=P, t=PACK)
@@ -98,337 +107,377 @@ def tile_aipwscorebasismoments_w8_kernel(tc, x, b, gam_words, gam_scales, lat, y
         v_rows = v_bytes.rearrange("(g p t) m -> g p t m", p=P, t=PACK)
         gam_flat = gam_words[0].rearrange("p n t -> p (n t)")
 
-        def load_x(j):
-            nc.sync.dma_start(out=x_raw[j][:], in_=x_rows[j // 2][:, 2 * (j % 2) : 2 * (j % 2) + 2, :])
+        def load_pair(dst, rows, j, width):
+            nc.sync.dma_start(out=dst[j][:], in_=rows[j // 2][:, 2 * (j % 2) : 2 * (j % 2) + 2, :width])
 
         def load_b(arm, part):
-            rows = b[arm].rearrange("(p j) q -> p j q", j=PACK)
+            rows = b[arm].rearrange("(p t) q -> p t q", t=PACK)
             nc.sync.dma_start(out=b_raw[arm * PARTS + part][:], in_=rows[:, :, part * PART : (part + 1) * PART])
 
-        nc.vector.memset(gam_s[:].bitcast(I32), 0)
-        nc.vector.memset(warm[:], 1.0)
-        nc.vector.tensor_scalar(out=ln_trim[:], in0=warm[:], scalar1=math.log(TRIM), scalar2=None, op0=ALU.mult)
+        def load_scores_first(j):
+            load_pair(lat_first, lat_rows, j, PART)
+            load_pair(y_first, y_rows, j, PART)
+
+        def load_scores_rest(g):
+            nc.sync.dma_start(out=lat_rest[g][:], in_=lat_rows[g][:, :, PART:])
+            nc.sync.dma_start(out=y_rest[g][:], in_=y_rows[g][:, :, PART:])
+
+        nc.vector.memset(gam_plane[:].bitcast(I32), 0)
+        nc.vector.memset(zero[:], 0.0)
         make_identity(nc, ident[:])
-        load_x(0)
+        make_identity(nc, ident_bf[:])
+
+        nc.sync.dma_start(out=v_fac[:], in_=v_scale.rearrange("(g p t) o -> p g (t o)", p=P, t=PACK))
+        load_pair(v_raw, v_rows, 0, M)
+        load_pair(x_raw, x_rows, 0, KX)
         load_b(1, 0)
         for quad in range(4):
             nc.scalar.dma_start(
-                out=gam_s[32 * quad : 32 * quad + 4, :].bitcast(I32),
+                out=gam_plane[32 * quad : 32 * quad + 4, :].bitcast(I32),
                 in_=gam_scales[0, 4 * quad : 4 * quad + 4, :].bitcast(I32),
             )
-        nc.scalar.activation(out=warm[:], in_=ln_trim[:], func=ACT.Exp)
+        nc.scalar.activation(out=one[:], in_=zero[:], func=ACT.Exp)
         nc.sync.dma_start(out=gam_first[:].bitcast(I32), in_=gam_flat[:, : PART * PACK].bitcast(I32))
-        load_x(1)
+        load_pair(v_raw, v_rows, 1, M)
+        load_pair(x_raw, x_rows, 1, KX)
         load_b(0, 0)
-        nc.sync.dma_start(out=y_first[0][:], in_=y_rows[0][:, :, :PART])
-        nc.sync.dma_start(out=lat_first[0][:], in_=lat_rows[0][:, :, :PART])
+        load_scores_first(0)
         nc.sync.dma_start(out=w_raw[:], in_=w.rearrange("(g p t) -> p g t", p=P, t=PACK))
-        load_x(2)
-        load_x(3)
-        nc.sync.dma_start(out=lat_first[1][:], in_=lat_rows[1][:, :, :PART])
-        nc.sync.dma_start(out=y_first[1][:], in_=y_rows[1][:, :, :PART])
+        load_pair(x_raw, x_rows, 2, KX)
+        load_scores_first(1)
+        load_pair(x_raw, x_rows, 3, KX)
         load_b(1, 1)
+        load_scores_first(2)
         load_b(0, 1)
-        nc.sync.dma_start(out=v_sc[:], in_=v_scale.rearrange("(g p t) o -> p g (t o)", p=P, t=PACK))
-        nc.sync.dma_start(out=v_raw[0][:], in_=v_rows[0])
+        load_scores_first(3)
         nc.sync.dma_start(out=gam_rest[:].bitcast(I32), in_=gam_flat[:, PART * PACK :].bitcast(I32))
-        nc.sync.dma_start(out=v_raw[1][:], in_=v_rows[1])
-        nc.sync.dma_start(out=lat_rest[0][:], in_=lat_rows[0][:, :, PART:])
-        nc.sync.dma_start(out=y_rest[0][:], in_=y_rows[0][:, :, PART:])
-        load_b(1, 2)
-        load_b(0, 2)
-        nc.sync.dma_start(out=lat_rest[1][:], in_=lat_rows[1][:, :, PART:])
-        nc.sync.dma_start(out=y_rest[1][:], in_=y_rows[1][:, :, PART:])
-        load_b(1, 3)
-        load_b(0, 3)
+        load_pair(v_raw, v_rows, 2, M)
+        load_pair(v_raw, v_rows, 3, M)
+        for g in range(GROUPS):
+            load_scores_rest(g)
+            load_b(1, 2 + g)
+            load_b(0, 2 + g)
 
         def quantize(codes, scales, src):
             nc.vector.quantize_mx(out=codes.bitcast(FP8X4), scales=scales, in_=src)
 
-        def interleave(on_vector, dst, src, scale):
+        def interleave(on_vector, dst, src, negate):
             dst_v = dst.rearrange("p (c i t) -> p c t i", i=RUN, t=PACK)
             src_v = src.rearrange("p t (c i) -> p c t i", i=RUN)
-            if on_vector and scale == 1.0:
-                nc.vector.tensor_copy(out=dst_v, in_=src_v)
+            if on_vector and negate:
+                nc.vector.tensor_scalar(out=dst_v, in0=src_v, scalar1=-1.0, scalar2=None, op0=ALU.mult)
             elif on_vector:
-                nc.vector.tensor_scalar(out=dst_v, in0=src_v, scalar1=scale, scalar2=None, op0=ALU.mult)
-            elif scale == 1.0:
-                nc.scalar.copy(out=dst_v, in_=src_v)
+                nc.vector.tensor_copy(out=dst_v, in_=src_v)
+            elif negate:
+                nc.scalar.activation(out=dst_v, in_=src_v, func=ACT.Copy, scale=-1.0)
             else:
-                nc.scalar.activation(out=dst_v, in_=src_v, func=ACT.Copy, scale=scale)
+                nc.scalar.copy(out=dst_v, in_=src_v)
 
         def x_turn(j):
             words = x_raw[j][:].rearrange("p a k -> p (a k)").bitcast(F32)
-            bank = o_ps[j % 2]
             half = KX // 2
             for a in range(2):
                 for u in range(2):
-                    nc.tensor.transpose(bank[:, (2 * a + u) * P : (2 * a + u + 1) * P], words[:, a * half + u : (a + 1) * half : 2], ident[:])
+                    nc.tensor.transpose(out_ps[j % 2][:, (2 * a + u) * P : (2 * a + u + 1) * P], words[:, a * half + u : (a + 1) * half : 2], ident[:])
 
         def x_copy(j):
             nc.scalar.copy(
-                out=x_il[j % 2][:].bitcast(F32).rearrange("p (a r u) -> p a r u", a=2, u=2),
-                in_=o_ps[j % 2][:].rearrange("p (a u r) -> p a r u", a=2, u=2),
+                out=x_woven[j % 2][:].bitcast(F32).rearrange("p (a r u) -> p a r u", a=2, u=2),
+                in_=out_ps[j % 2][:].rearrange("p (a u r) -> p a r u", a=2, u=2),
             )
 
         def x_quant(j):
-            quantize(x_c[j][:], x_s[j][:], x_il[j % 2][:])
+            quantize(x_codes[j][:], x_scales[j][:], x_woven[j % 2][:])
 
         def x_operand(g, t):
-            j = 2 * g + t // 2
             cols = slice((t % 2) * P, (t % 2 + 1) * P)
-            return x_c[j][:, cols].bitcast(FP8X4), x_s[j][:, cols]
+            return x_codes[2 * g + t // 2][:, cols].bitcast(FP8X4), x_scales[2 * g + t // 2][:, cols]
 
         def b_operand(arm, col0, width):
-            k = arm * PARTS + col0 // PART
             cols = slice(col0 % PART, col0 % PART + width)
-            return b_c[k][:, cols].bitcast(FP8X4), b_s[k][:, cols]
+            return b_codes[arm * PARTS + col0 // PART][:, cols].bitcast(FP8X4), b_scales[arm * PARTS + col0 // PART][:, cols]
 
         def gam_operand(col0, width):
-            if col0 < PART:
-                codes = gam_first[:, col0 : col0 + width]
-            else:
-                codes = gam_rest[:, col0 - PART : col0 - PART + width]
-            return codes.bitcast(FP8X4), gam_s[:, col0 : col0 + width]
+            codes = gam_first[:, col0 : col0 + width] if col0 < PART else gam_rest[:, col0 - PART : col0 - PART + width]
+            return codes.bitcast(FP8X4), gam_plane[:, col0 : col0 + width]
 
-        def stage1(bank, s, movers):
+        def rows_times(bank, s, movers):
             col0, width, g, t0, count = units[s]
             for i in range(count):
-                lhs, lhs_s = x_operand(g, t0 + i)
-                for n, (rhs, rhs_s) in enumerate(movers):
-                    nc.tensor.matmul_mx(out=bank[:, i * width : (i + 1) * width], lhsT=lhs, lhsT_scale=lhs_s, rhs=rhs, rhs_scale=rhs_s,
+                lhs, lhs_scale = x_operand(g, t0 + i)
+                for n, (rhs, rhs_scale) in enumerate(movers):
+                    nc.tensor.matmul_mx(out=bank[:, i * width : (i + 1) * width], lhsT=lhs, lhsT_scale=lhs_scale, rhs=rhs, rhs_scale=rhs_scale,
                                         start=(n == 0), stop=(n == len(movers) - 1))
 
         def mm_z(s):
-            stage1(z_ps[s % 2], s, [gam_operand(units[s][0], units[s][1])])
+            rows_times(z_ps[s % 2], s, [gam_operand(units[s][0], units[s][1])])
+
+        def mm_diff(s):
+            rows_times(diff_ps, s, [b_operand(1, units[s][0], units[s][1]), b_operand(0, units[s][0], units[s][1])])
 
         def mm_mu(s):
-            stage1(mu_ps[s % 2], s, [b_operand(1, units[s][0], units[s][1])])
+            col0, width, g, t0, count = units[s]
+            for i in range(2):
+                block, t = divmod(2 * i, count)
+                lhs, lhs_scale = b_operand(1, col0 + block * P, P)
+                pair = 2 * g + (t0 + t) // 2
+                nc.tensor.matmul_mx(out=mu_ps[:, i * 2 * P : (i + 1) * 2 * P], lhsT=lhs, lhsT_scale=lhs_scale,
+                                    rhs=x_codes[pair][:].bitcast(FP8X4), rhs_scale=x_scales[pair][:], start=True, stop=True)
 
-        def mm_d(s):
-            stage1(d_ps[s % 2], s, [b_operand(1, units[s][0], units[s][1]), b_operand(0, units[s][0], units[s][1])])
+        def mu_out(s):
+            nc.scalar.activation(out=mu_neg[s % 2][:], in_=mu_ps[:], func=ACT.Copy, scale=-1.0)
 
         def rows_of(first, rest, s):
             col0, width, g, t0, count = units[s]
             if col0 < PART:
-                return first[g][:, t0 : t0 + count, col0 : col0 + width]
+                return first[2 * g + t0 // 2][:]
             return rest[g][:, t0 : t0 + count, col0 - PART : col0 - PART + width]
 
-        def by_t(tile_ap, s):
-            return tile_ap.rearrange("p (t c) -> p t c", t=units[s][4])
+        def by_t(flat, s):
+            return flat.rearrange("p (t c) -> p t c", t=units[s][4])
+
+        def mm_resid(s):
+            col0, width, g, t0, count = units[s]
+            bank = resid_ps[s % 2]
+            nc.tensor.matmul(out=by_t(bank[:], s), lhsT=ident_bf[:], rhs=rows_of(y_first, y_rest, s), start=True, stop=False)
+            for i in range(BANK // P):
+                block, t = divmod(i, count)
+                at = t * width + block * P
+                nc.tensor.matmul(out=bank[:, at : at + P], lhsT=mu_neg[s % 2][:, i * P : (i + 1) * P], rhs=ident[:],
+                                 is_transpose=True, start=False, stop=(i == BANK // P - 1))
 
         def exps(s):
-            nc.scalar.activation(out=f_t[s % 4][:], in_=z_ps[s % 2][:], func=ACT.Exp, scale=-1.0)
-            nc.scalar.activation(out=e_t[s % 4][:], in_=z_ps[s % 2][:], func=ACT.Exp, bias=ln_trim[:])
+            nc.scalar.activation(out=exp_neg[s % EXP_DEPTH][:], in_=z_ps[s % 2][:], func=ACT.Exp, scale=-1.0)
+            nc.scalar.activation(out=exp_pos[s % EXP_DEPTH][:], in_=z_ps[s % 2][:], func=ACT.Exp, bias=ln_trim[:])
 
-        def op_mask(s):
-            nc.vector.tensor_scalar(out=by_t(n_t[s % 3][:], s), in0=rows_of(lat_first, lat_rest, s), scalar1=0.0, scalar2=TRIM,
+        def op_cap(s):
+            nc.vector.tensor_scalar(out=by_t(cap[s % MID_DEPTH][:], s), in0=rows_of(lat_first, lat_rest, s), scalar1=0.0, scalar2=TRIM,
                                     op0=ALU.is_le, op1=ALU.subtract)
 
         def op_clip(s):
-            nc.vector.tensor_scalar(out=f_t[s % 4][:], in0=f_t[s % 4][:], scalar1=ODDS_LO, scalar2=ODDS_HI, op0=ALU.max, op1=ALU.min)
-
-        def op_resid(s):
-            nc.vector.tensor_tensor(out=by_t(a_t[s % 3][:], s), in0=rows_of(y_first, y_rest, s), in1=by_t(mu_ps[s % 2][:], s), op=ALU.subtract)
+            f = exp_neg[s % EXP_DEPTH]
+            nc.vector.tensor_scalar(out=f[:], in0=f[:], scalar1=ODDS_LO, scalar2=ODDS_HI, op0=ALU.max, op1=ALU.min)
 
         def op_weigh(s):
-            nc.vector.scalar_tensor_tensor(out=a_t[s % 3][:], in0=f_t[s % 4][:], scalar=1.0, in1=a_t[s % 3][:], op0=ALU.add, op1=ALU.mult)
+            nc.vector.scalar_tensor_tensor(out=acc[s % MID_DEPTH][:], in0=exp_neg[s % EXP_DEPTH][:], scalar=1.0, in1=resid_ps[s % 2][:],
+                                           op0=ALU.add, op1=ALU.mult)
 
         def op_contrast(s):
-            nc.vector.tensor_tensor(out=a_t[s % 3][:], in0=a_t[s % 3][:], in1=d_ps[s % 2][:], op=ALU.add)
+            nc.vector.tensor_tensor(out=acc[s % MID_DEPTH][:], in0=acc[s % MID_DEPTH][:], in1=diff_ps[:], op=ALU.add)
 
         def op_arm(s):
-            nc.vector.scalar_tensor_tensor(out=e_t[s % 4][:], in0=e_t[s % 4][:], scalar=TRIM * ODDS_LO, in1=n_t[s % 3][:], op0=ALU.max, op1=ALU.min)
-
-        def block_of(s):
-            return len([1 for r in range(s) if units[r][3] + units[r][4] == PACK])
-
-        def op_score(s):
-            col0, width, g, t0, count = units[s]
-            for i in range(count):
-                t = t0 + i
-                cols = slice(i * width, (i + 1) * width)
-                nc.vector.scalar_tensor_tensor(out=g_rows[block_of(s) % 2][:, t, :width], in0=a_t[s % 3][:, cols],
-                                               scalar=w_neg[:, g * PACK + t : g * PACK + t + 1], in1=e_t[s % 4][:, cols],
-                                               op0=ALU.mult, op1=ALU.mult)
+            e = exp_pos[s % EXP_DEPTH]
+            nc.vector.scalar_tensor_tensor(out=e[:], in0=e[:], scalar=TRIM * ODDS_LO, in1=cap[s % MID_DEPTH][:], op0=ALU.max, op1=ALU.min)
 
         def closes_block(s):
             return units[s][3] + units[s][4] == PACK
 
+        def block_slot(s):
+            return len([r for r in range(s) if closes_block(r)]) % 2
+
+        def op_score(s):
+            col0, width, g, t0, count = units[s]
+            for i in range(count):
+                cols = slice(i * width, (i + 1) * width)
+                row = g * PACK + t0 + i
+                nc.vector.scalar_tensor_tensor(out=g_rows[block_slot(s)][:, t0 + i, :width], in0=acc[s % MID_DEPTH][:, cols],
+                                               scalar=w_fac[:, row : row + 1], in1=exp_pos[s % EXP_DEPTH][:, cols], op0=ALU.mult, op1=ALU.mult)
+
         def g_weave(s, on_vector):
             width = units[s][1]
-            interleave(on_vector, g_il[block_of(s) % 2][:, : width * PACK], g_rows[block_of(s) % 2][:, :, :width], 1.0)
+            interleave(on_vector, g_woven[block_slot(s)][:, : width * PACK], g_rows[block_slot(s)][:, :, :width], False)
+
+        g_done = []
+        v_done = []
+        weaves = []
 
         def g_quant(s):
             col0, width, g, t0, count = units[s]
-            quantize(g_c[g][:, col0 : col0 + width], g_s[g][:, col0 : col0 + width], g_il[block_of(s) % 2][:, : width * PACK])
-
-        slot = []
+            quantize(g_codes[g][:, col0 : col0 + width], g_scales[g][:, col0 : col0 + width], g_woven[block_slot(s)][:, : width * PACK])
+            g_done.append((col0, g))
 
         def b_weave(arm, part, on_vector):
-            buf = il[len(slot) % 4]
-            slot.append(1)
-            interleave(on_vector, buf[:], b_raw[arm * PARTS + part][:], 1.0 if arm == 1 else -1.0)
-            return lambda: quantize(b_c[arm * PARTS + part][:], b_s[arm * PARTS + part][:], buf[:])
+            buf = woven[len(weaves) % WEAVE_DEPTH]
+            weaves.append(buf)
+            interleave(on_vector, buf[:], b_raw[arm * PARTS + part][:], arm == 0)
+            return lambda: quantize(b_codes[arm * PARTS + part][:], b_scales[arm * PARTS + part][:], buf[:])
 
         def v_widen(g, t, on_vector):
+            src = v_raw[2 * g + t // 2][:, t % 2, :].bitcast(FP8)
             if on_vector:
-                nc.vector.tensor_scalar(out=v_wide[g][:, t, :], in0=v_raw[g][:, t, :].bitcast(FP8), scalar1=v_sc[:, g, t : t + 1], scalar2=None, op0=ALU.mult)
+                nc.vector.tensor_scalar(out=v_wide[g][:, t, :], in0=src, scalar1=v_fac[:, g, t : t + 1], scalar2=None, op0=ALU.mult)
             else:
-                nc.scalar.activation(out=v_wide[g][:, t, :], in_=v_raw[g][:, t, :].bitcast(FP8), func=ACT.Copy, scale=v_sc[:, g, t : t + 1])
+                nc.scalar.activation(out=v_wide[g][:, t, :], in_=src, func=ACT.Copy, scale=v_fac[:, g, t : t + 1])
 
         def v_weave(g, part, on_vector):
-            buf = il[len(slot) % 4]
-            slot.append(1)
+            buf = woven[len(weaves) % WEAVE_DEPTH]
+            weaves.append(buf)
             cols = slice(part * PART, (part + 1) * PART)
-            interleave(on_vector, buf[:], v_wide[g][:, :, cols], 1.0)
-            return lambda: quantize(v_c[g][:, cols], v_s[g][:, cols], buf[:])
+            interleave(on_vector, buf[:], v_wide[g][:, :, cols], False)
 
-        outs = []
-        col = 0
-        for width in CHUNKS:
-            for j0 in range(0, M // P, BANK // width):
-                outs.append((col, width, j0))
-            col = col + width
+            def v_quant():
+                quantize(v_codes[g][:, cols], v_scales[g][:, cols], buf[:])
+                v_done.append((g, part))
 
-        def mm_out(k):
-            col0, width, j0 = outs[k]
-            for i in range(BANK // width):
-                m_cols = slice((j0 + i) * P, (j0 + i + 1) * P)
-                for g in range(GROUPS):
-                    nc.tensor.matmul_mx(out=o_ps[k % 2][:, i * width : (i + 1) * width], lhsT=v_c[g][:, m_cols].bitcast(FP8X4), lhsT_scale=v_s[g][:, m_cols],
-                                        rhs=g_c[g][:, col0 : col0 + width].bitcast(FP8X4), rhs_scale=g_s[g][:, col0 : col0 + width],
-                                        start=(g == 0), stop=(g == GROUPS - 1))
+            return v_quant
 
-        def copy_out(k, on_vector, queue):
-            col0, width, j0 = outs[k]
-            count = BANK // width
+        def out_pass(dst, j, col0, width, g):
+            rows = slice(j * P, (j + 1) * P)
+            cols = slice(col0, col0 + width)
+            nc.tensor.matmul_mx(out=dst, lhsT=v_codes[g][:, rows].bitcast(FP8X4), lhsT_scale=v_scales[g][:, rows],
+                                rhs=g_codes[g][:, cols].bitcast(FP8X4), rhs_scale=g_scales[g][:, cols], start=(g == 0), stop=(g == GROUPS - 1))
+
+        def out_scale(on_vector, dst, src):
             if on_vector:
-                nc.vector.tensor_scalar(out=o_t[k % 8][:], in0=o_ps[k % 2][:], scalar1=1.0 / math.sqrt(N), scalar2=None, op0=ALU.mult)
+                nc.vector.tensor_scalar(out=dst, in0=src, scalar1=1.0 / math.sqrt(N), scalar2=None, op0=ALU.mult)
             else:
-                nc.scalar.activation(out=o_t[k % 8][:], in_=o_ps[k % 2][:], func=ACT.Copy, scale=1.0 / math.sqrt(N))
+                nc.scalar.activation(out=dst, in_=src, func=ACT.Copy, scale=1.0 / math.sqrt(N))
+
+        def out_store(src, j0, count, col0, width):
             dst = out[j0 * P : (j0 + count) * P, col0 : col0 + width].rearrange("(j p) q -> p j q", p=P)
-            queue.dma_start(out=dst, in_=o_t[k % 8][:].rearrange("p (j q) -> p j q", j=count))
+            nc.sync.dma_start(out=dst, in_=src.rearrange("p (j q) -> p j q", j=count))
+
+        filled = []
+        emptied = []
+        looped = len(outs) - M // P * CHUNKS[-1] // BANK
+
+        def fill_outs():
+            while len(filled) < min(len(emptied) + 2, looped):
+                col0, width, j0 = outs[len(filled)]
+                count = BANK // width
+                parts = range(j0 * P // PART, ((j0 + count) * P - 1) // PART + 1)
+                if not all((col0, g) in g_done and (g, part) in v_done for g in range(GROUPS) for part in parts):
+                    break
+                for i in range(count):
+                    for g in range(GROUPS):
+                        out_pass(out_ps[len(filled) % 2][:, i * width : (i + 1) * width], j0 + i, col0, width, g)
+                filled.append(j0)
+
+        def empty_outs(most):
+            for n in range(most):
+                if len(emptied) < len(filled):
+                    k = len(emptied)
+                    col0, width, j0 = outs[k]
+                    out_scale(False, stage[k % STAGE_DEPTH][:], out_ps[k % 2][:])
+                    out_store(stage[k % STAGE_DEPTH][:], j0, BANK // width, col0, width)
+                    emptied.append(j0)
+                    fill_outs()
 
         x_turn(0)
+        v_widen(0, 0, False)
+        v_widen(0, 1, True)
+        nc.vector.tensor_scalar(out=ln_trim[:], in0=one[:], scalar1=math.log(TRIM), scalar2=None, op0=ALU.mult)
         x_copy(0)
-        x_turn(1)
         quant_b1 = b_weave(1, 0, True)
-        x_quant(0)
+        v_widen(0, 2, False)
         quant_b1()
-        mm_z(0)
+        x_quant(0)
         mm_mu(0)
-        x_copy(1)
+        mm_z(0)
+        x_turn(1)
+        v_widen(0, 3, True)
+        mu_out(0)
         exps(0)
+        x_copy(1)
         quant_b0 = b_weave(0, 0, True)
-        x_quant(1)
+        op_cap(0)
         quant_b0()
-        mm_z(1)
-        mm_d(0)
-        mm_mu(1)
-        x_turn(2)
-        x_turn(3)
-        exps(1)
-        x_copy(2)
-        x_copy(3)
-        op_resid(0)
-        op_mask(0)
         op_clip(0)
-        nc.vector.tensor_scalar(out=w_neg[:], in0=w_raw[:].rearrange("p g t -> p (g t)"), scalar1=-1.0 / TRIM, scalar2=None, op0=ALU.mult)
+        nc.vector.tensor_scalar(out=w_fac[:], in0=w_raw[:].rearrange("p g t -> p (g t)"), scalar1=-1.0 / TRIM, scalar2=None, op0=ALU.mult)
+        mm_resid(0)
+        mm_diff(0)
+        x_turn(2)
+        quant_v0 = v_weave(0, 0, True)
+        x_quant(1)
+        mm_mu(1)
+        mm_z(1)
+        quant_v1 = v_weave(0, 1, False)
+        x_copy(2)
+        mu_out(1)
+        exps(1)
+        x_turn(3)
+        x_copy(3)
         op_arm(0)
-        op_mask(1)
+        quant_v0()
+        op_cap(1)
+        quant_v2 = v_weave(0, 2, True)
+        quant_v1()
         x_quant(2)
-        x_quant(3)
+        mm_mu(2)
         mm_z(2)
 
-        SIDE = [
-            [("b", 1, 1, False), ("b", 0, 1, False)],
-            [("vw", 0, 0, False), ("vw", 0, 1, False), ("vw", 0, 2, False)],
-            [("vw", 0, 3, False), ("vw", 1, 0, False)],
-            [("vw", 1, 1, False), ("vw", 1, 2, False), ("vw", 1, 3, False)],
-            [("b", 1, 2, False)],
-            [("b", 0, 2, False), ("vi", 0, 0, False)],
-            [("vi", 1, 0, False)],
-            [("vi", 0, 1, False), ("vi", 1, 1, False)],
-            [("b", 1, 3, False)],
-            [("b", 0, 3, False), ("vi", 0, 2, False)],
-            [("vi", 1, 2, False)],
-            [("vi", 0, 3, False), ("vi", 1, 3, False)],
-            [("o", 3, False)] * 3,
-            [("o", 12, False)] * 4,
-            [("o", 12, False)] * 5,
-            [("o", 14, False)] * 2,
-        ]
-
-        pending = []
-        made = 0
-        copied = 0
+        wide_steps = BANK // CHUNKS[0] * GROUPS
+        due = [quant_v2, lambda: x_quant(3)]
         for s in range(len(units)):
-            if s + 3 <= last:
-                pass_z = s + 3
-            else:
-                pass_z = None
-            if s + 2 <= last:
-                exps(s + 2)
-            if pass_z is not None:
-                mm_z(pass_z)
-            if s + 2 <= last:
-                mm_mu(s + 2)
-            if s + 1 <= last:
-                mm_d(s + 1)
-            quants = pending
-            pending = []
-            on_dve = []
-            if s >= 1 and closes_block(s - 1):
+            quants = due
+            due = []
+            room = SCALAR_ROOM
+            late = s + 2 > last
+            settled = s >= 2
+            block_closed = s >= 1 and closes_block(s - 1)
+            if block_closed and late:
                 g_weave(s - 1, False)
-                quants.append(lambda r=s - 1: g_quant(r))
-            for job in SIDE[s]:
-                if job[-1]:
-                    on_dve.append(job)
-                elif job[0] == "b":
-                    pending.append(b_weave(job[1], job[2], False))
-                elif job[0] == "vw":
-                    v_widen(job[1], job[2], False)
-                elif job[0] == "vi":
-                    pending.append(v_weave(job[1], job[2], False))
-                else:
-                    while made < min(copied + 2, job[1]):
-                        mm_out(made)
-                        made = made + 1
-                    copy_out(copied, False, nc.sync)
-                    copied = copied + 1
-                    if made < job[1]:
-                        mm_out(made)
-                        made = made + 1
+            if s + 1 <= last:
+                mm_resid(s + 1)
+            if not late:
+                mu_out(s + 2)
+            if settled and s + 3 <= last:
+                mm_mu(s + 3)
             if s + 1 <= last:
                 op_clip(s + 1)
             op_weigh(s)
-            if s + 1 <= last:
-                op_resid(s + 1)
-            op_contrast(s)
+            if not late:
+                exps(s + 2)
+                room = room - 3
+            if settled and s + 3 <= last:
+                mm_z(s + 3)
             if s + 1 <= last:
                 op_arm(s + 1)
+            op_contrast(s)
+            if block_closed:
+                if not late:
+                    g_weave(s - 1, False)
+                (quants if late else due).append(lambda r=s - 1: g_quant(r))
+                room = room - units[s - 1][1] * PACK // BANK
+            for part in range(1, PARTS):
+                if s == max(0, wide_steps * part - 5):
+                    due.append(b_weave(1, part, False))
+                    room = room - 2
+                if s == wide_steps * part - 3:
+                    due.append(b_weave(0, part, False))
+                    room = room - 2
+            if s == 1:
+                due.append(v_weave(0, PARTS - 1, False))
+            if PACK <= s < PACK + PARTS and s % 2 == 0:
+                due.append(v_weave(1, s - PACK, False))
+                room = room - 2
+            empty_outs(room)
+            if s + 1 <= last:
+                mm_diff(s + 1)
+            if not late:
+                op_cap(s + 2)
             op_score(s)
-            if s + 2 <= last:
-                op_mask(s + 2)
-            for job in on_dve:
-                if job[0] == "vw":
-                    v_widen(job[1], job[2], True)
-                elif job[0] == "vi":
-                    pending.append(v_weave(job[1], job[2], True))
-                else:
-                    pending.append(b_weave(job[1], job[2], True))
+            if s < PACK:
+                v_widen(1, s, True)
+            if PACK <= s < PACK + PARTS and s % 2 == 1:
+                due.append(v_weave(1, s - PACK, True))
             for run in quants:
                 run()
+            if not settled:
+                mm_mu(s + 3)
+                mm_z(s + 3)
+            fill_outs()
 
-        for run in pending:
-            run()
+        empty_outs(looped - len(emptied))
+        col0, width = units[last][:2]
+        spare = z_ps + [mu_ps] + resid_ps + [diff_ps] + out_ps
+        for j in range(M // P):
+            out_pass(spare[j][:, :width], j, col0, width, 0)
         g_weave(last, True)
         g_quant(last)
-        while copied < len(outs):
-            while made < min(copied + 2, len(outs)):
-                mm_out(made)
-                made = made + 1
-            at_end = copied == len(outs) - 1
-            copy_out(copied, at_end, nc.sync if (at_end or copied < len(outs) - 2) else nc.scalar)
-            copied = copied + 1
+        for j in range(M // P):
+            out_pass(spare[j][:, :width], j, col0, width, 1)
+            both = stage[(looped + j // 2) % STAGE_DEPTH]
+            out_scale(j % 2 == 1, both[:, (j % 2) * width : (j % 2 + 1) * width], spare[j][:, :width])
+            if j % 2 == 1:
+                out_store(both[:, : 2 * width], j - 1, 2, col0, width)

@@ -30,6 +30,8 @@ ODDS_LO = TRIM / (1.0 - TRIM)
 ODDS_HI = (1.0 - TRIM) / TRIM
 RUN = 4
 SCALAR_ROOM = 6
+G_ON_VECTOR = 6
+TURNS = 7
 EXP_DEPTH = 4
 MID_DEPTH = 3
 WEAVE_DEPTH = 6
@@ -173,6 +175,16 @@ def tile_aipwscorebasismoments_w8_kernel(tc, x, b, gam_words, gam_scales, lat, y
             else:
                 nc.scalar.copy(out=dst_v, in_=src_v)
 
+        turned = []
+
+        def turn(src):
+            bank = out_ps[len(turned) % 2][:].bitcast(BF16)
+            turned.append(bank)
+            for h in range(PART // P):
+                nc.tensor.matmul(out=bank[:, h * BANK : (h + 1) * BANK].rearrange("p (c t) -> p c t", t=PACK), lhsT=ident_bf[:],
+                                 rhs=src[:, :, h * P : (h + 1) * P].rearrange("p t c -> p c t"), start=True, stop=True)
+            return bank
+
         def x_turn(j):
             words = x_raw[j][:].rearrange("p a k -> p (a k)").bitcast(F32)
             half = KX // 2
@@ -258,12 +270,17 @@ def tile_aipwscorebasismoments_w8_kernel(tc, x, b, gam_words, gam_scales, lat, y
             f = exp_neg[s % EXP_DEPTH]
             nc.vector.tensor_scalar(out=f[:], in0=f[:], scalar1=ODDS_LO, scalar2=ODDS_HI, op0=ALU.max, op1=ALU.min)
 
+        def spans(s):
+            return [slice(0, BANK // 2), slice(BANK // 2, BANK)] if s == last else [slice(0, BANK)]
+
         def op_weigh(s):
-            nc.vector.scalar_tensor_tensor(out=acc[s % MID_DEPTH][:], in0=exp_neg[s % EXP_DEPTH][:], scalar=1.0, in1=resid_ps[s % 2][:],
-                                           op0=ALU.add, op1=ALU.mult)
+            for cols in spans(s):
+                nc.vector.scalar_tensor_tensor(out=acc[s % MID_DEPTH][:, cols], in0=exp_neg[s % EXP_DEPTH][:, cols], scalar=1.0,
+                                               in1=resid_ps[s % 2][:, cols], op0=ALU.add, op1=ALU.mult)
 
         def op_contrast(s):
-            nc.vector.tensor_tensor(out=acc[s % MID_DEPTH][:], in0=acc[s % MID_DEPTH][:], in1=diff_ps[:], op=ALU.add)
+            for cols in spans(s):
+                nc.vector.tensor_tensor(out=acc[s % MID_DEPTH][:, cols], in0=acc[s % MID_DEPTH][:, cols], in1=diff_ps[:, cols], op=ALU.add)
 
         def op_arm(s):
             e = exp_pos[s % EXP_DEPTH]
@@ -296,10 +313,13 @@ def tile_aipwscorebasismoments_w8_kernel(tc, x, b, gam_words, gam_scales, lat, y
             quantize(g_codes[g][:, col0 : col0 + width], g_scales[g][:, col0 : col0 + width], g_woven[block_slot(s)][:, : width * PACK])
             g_done.append((col0, g))
 
-        def b_weave(arm, part, on_vector):
+        def b_weave(arm, part, on_vector, bank=None):
             buf = woven[len(weaves) % WEAVE_DEPTH]
             weaves.append(buf)
-            interleave(on_vector, buf[:], b_raw[arm * PARTS + part][:], arm == 0)
+            if bank is None:
+                interleave(on_vector, buf[:], b_raw[arm * PARTS + part][:], arm == 0)
+            else:
+                nc.scalar.copy(out=buf[:], in_=bank)
             return lambda: quantize(b_codes[arm * PARTS + part][:], b_scales[arm * PARTS + part][:], buf[:])
 
         def v_widen(g, t, on_vector):
@@ -309,11 +329,14 @@ def tile_aipwscorebasismoments_w8_kernel(tc, x, b, gam_words, gam_scales, lat, y
             else:
                 nc.scalar.activation(out=v_wide[g][:, t, :], in_=src, func=ACT.Copy, scale=v_fac[:, g, t : t + 1])
 
-        def v_weave(g, part, on_vector):
+        def v_weave(g, part, on_vector, bank=None):
             buf = woven[len(weaves) % WEAVE_DEPTH]
             weaves.append(buf)
             cols = slice(part * PART, (part + 1) * PART)
-            interleave(on_vector, buf[:], v_wide[g][:, :, cols], False)
+            if bank is None:
+                interleave(on_vector, buf[:], v_wide[g][:, :, cols], False)
+            else:
+                nc.scalar.copy(out=buf[:], in_=bank)
 
             def v_quant():
                 quantize(v_codes[g][:, cols], v_scales[g][:, cols], buf[:])
@@ -342,7 +365,7 @@ def tile_aipwscorebasismoments_w8_kernel(tc, x, b, gam_words, gam_scales, lat, y
         looped = len(outs) - M // P * CHUNKS[-1] // BANK
 
         def fill_outs():
-            while len(filled) < min(len(emptied) + 2, looped):
+            while len(turned) == TURNS and len(filled) < min(len(emptied) + 2, looped):
                 col0, width, j0 = outs[len(filled)]
                 count = BANK // width
                 parts = range(j0 * P // PART, ((j0 + count) * P - 1) // PART + 1)
@@ -419,6 +442,10 @@ def tile_aipwscorebasismoments_w8_kernel(tc, x, b, gam_words, gam_scales, lat, y
                 g_weave(s - 1, False)
             if s + 1 <= last:
                 mm_resid(s + 1)
+            b_parts = [part for part in range(1, PARTS) if s == max(0, wide_steps * part - 5)]
+            v_parts = [(0, PARTS - 1)] if s == 1 else [(1, s - PACK + 1)] if PACK - 1 <= s < PACK - 1 + PARTS else []
+            b_banks = [turn(b_raw[PARTS + part][:]) if part < PARTS - 1 else None for part in b_parts]
+            v_banks = [turn(v_wide[g][:, :, part * PART : (part + 1) * PART]) for g, part in v_parts]
             if not late:
                 mu_out(s + 2)
             if settled and s + 3 <= last:
@@ -435,32 +462,35 @@ def tile_aipwscorebasismoments_w8_kernel(tc, x, b, gam_words, gam_scales, lat, y
                 op_arm(s + 1)
             op_contrast(s)
             if block_closed:
-                if not late:
+                if not late and s != G_ON_VECTOR:
                     g_weave(s - 1, False)
                 (quants if late else due).append(lambda r=s - 1: g_quant(r))
-                room = room - units[s - 1][1] * PACK // BANK
+                if s != G_ON_VECTOR:
+                    room = room - units[s - 1][1] * PACK // BANK
+            for part, bank in zip(b_parts, b_banks):
+                due.append(b_weave(1, part, False, bank))
+                room = room - 2
+            for (g, part), bank in zip(v_parts, v_banks):
+                due.append(v_weave(g, part, False, bank))
             for part in range(1, PARTS):
-                if s == max(0, wide_steps * part - 5):
-                    due.append(b_weave(1, part, False))
-                    room = room - 2
                 if s == wide_steps * part - 3:
                     due.append(b_weave(0, part, False))
                     room = room - 2
-            if s == 1:
-                due.append(v_weave(0, PARTS - 1, False))
-            if PACK <= s < PACK + PARTS and s % 2 == 0:
-                due.append(v_weave(1, s - PACK, False))
-                room = room - 2
+            v_rows_now = [t for t in range(PACK) if s == min(t, 2)]
+            for t in v_rows_now:
+                if t not in (1, 2):
+                    v_widen(1, t, False)
             empty_outs(room)
             if s + 1 <= last:
                 mm_diff(s + 1)
             if not late:
                 op_cap(s + 2)
+            if s == G_ON_VECTOR:
+                g_weave(s - 1, True)
             op_score(s)
-            if s < PACK:
-                v_widen(1, s, True)
-            if PACK <= s < PACK + PARTS and s % 2 == 1:
-                due.append(v_weave(1, s - PACK, True))
+            for t in v_rows_now:
+                if t in (1, 2):
+                    v_widen(1, t, True)
             for run in quants:
                 run()
             if not settled:

import math
from contextlib import ExitStack

import concourse.mybir as mybir
from concourse.masks import make_identity

N, KX, Q, M = 1024, 512, 1024, 1024
FLOPS = 2 * N * KX * Q * 3 + 2 * N * M * Q

F32 = mybir.dt.float32
BF16 = mybir.dt.bfloat16
I32 = mybir.dt.int32
U32 = mybir.dt.uint32
U8 = mybir.dt.uint8
FP8 = mybir.dt.float8_e4m3fn
FP8X4 = mybir.dt.float8_e4m3fn_x4
ALU = mybir.AluOpType
ACT = mybir.ActivationFunctionType

P = 128
PACK = 4
BANK = 512
GROUPS = N // (P * PACK)
PAIRS = GROUPS * PACK // 2
PART = 256
PARTS = Q // PART
CHUNKS = [256, 256, 256, 128, 128]
TRIM = 0.15
ODDS_LO = TRIM / (1.0 - TRIM)
ODDS_HI = (1.0 - TRIM) / TRIM
RUN = 4
SCALAR_ROOM = 6
G_ON_VECTOR = 6
TURNS = 7
EXP_DEPTH = 4
MID_DEPTH = 3
WEAVE_DEPTH = 6
STAGE_DEPTH = 8


def tile_aipwscorebasismoments_w8_kernel(tc, x, b, gam_words, gam_scales, lat, y, v_bytes, v_scale, w, out):
    nc = tc.nc
    with ExitStack() as ctx:
        sb = ctx.enter_context(tc.tile_pool(name="sb", bufs=1))
        ps = ctx.enter_context(tc.psum_pool(name="ps", bufs=1))
        ctx.enter_context(tc.manual_schedule())

        def tiles(label, count, shape, dtype):
            return [sb.tile(shape, dtype, name="%s%d" % (label, i), align_bytes=64) for i in range(count)]

        def banks(label, count):
            return [ps.tile([P, BANK], F32, name="%s%d" % (label, i)) for i in range(count)]

        ident = sb.tile([P, P], F32, name="ident")
        ident_bf = sb.tile([P, P], BF16, name="ident_bf")
        ln_trim = sb.tile([P, 1], F32, name="ln_trim")
        zero = sb.tile([P, 1], F32, name="zero")
        one = sb.tile([P, 1], F32, name="one")
        w_raw = sb.tile([P, GROUPS, PACK], BF16, name="w_raw")
        w_fac = sb.tile([P, GROUPS * PACK], F32, name="w_fac")
        v_fac = sb.tile([P, GROUPS, PACK], F32, name="v_fac")
        x_raw = tiles("x_raw", PAIRS, [P, 2, KX], BF16)
        x_woven = tiles("x_woven", 2, [P, 2 * P * PACK], BF16)
        x_codes = tiles("x_codes", PAIRS, [P, 2 * P], U32)
        x_scales = tiles("x_scales", PAIRS, [P, 2 * P], U8)
        b_raw = tiles("b_raw", 2 * PARTS, [P, PACK, PART], BF16)
        b_codes = tiles("b_codes", 2 * PARTS, [P, PART], U32)
        b_scales = tiles("b_scales", 2 * PARTS, [P, PART], U8)
        woven = tiles("woven", WEAVE_DEPTH, [P, PART * PACK], BF16)
        gam_first = sb.tile([P, PART], U32, name="gam_first", align_bytes=64)
        gam_rest = sb.tile([P, Q - PART], U32, name="gam_rest", align_bytes=64)
        gam_plane = sb.tile([P, Q], U8, name="gam_plane", align_bytes=64)
        lat_first = tiles("lat_first", PAIRS, [P, 2, PART], BF16)
        lat_rest = tiles("lat_rest", GROUPS, [P, PACK, Q - PART], BF16)
        y_first = tiles("y_first", PAIRS, [P, 2, PART], BF16)
        y_rest = tiles("y_rest", GROUPS, [P, PACK, Q - PART], BF16)
        v_raw = tiles("v_raw", PAIRS, [P, 2, M], U8)
        v_wide = tiles("v_wide", GROUPS, [P, PACK, M], BF16)
        v_codes = tiles("v_codes", GROUPS, [P, M], U32)
        v_scales = tiles("v_scales", GROUPS, [P, M], U8)
        g_rows = tiles("g_rows", 2, [P, PACK, PART], BF16)
        g_woven = tiles("g_woven", 2, [P, PART * PACK], BF16)
        g_codes = tiles("g_codes", GROUPS, [P, Q], U32)
        g_scales = tiles("g_scales", GROUPS, [P, Q], U8)
        exp_neg = tiles("exp_neg", EXP_DEPTH, [P, BANK], F32)
        exp_pos = tiles("exp_pos", EXP_DEPTH, [P, BANK], F32)
        cap = tiles("cap", MID_DEPTH, [P, BANK], F32)
        acc = tiles("acc", MID_DEPTH, [P, BANK], F32)
        stage = tiles("stage", STAGE_DEPTH, [P, BANK], F32)
        z_ps = banks("z_ps", 2)
        mu_ps = ps.tile([P, BANK], F32, name="mu_ps")
        resid_ps = banks("resid_ps", 2)
        diff_ps = ps.tile([P, BANK], F32, name="diff_ps")
        mu_neg = tiles("mu_neg", 2, [P, BANK], F32)
        out_ps = banks("out_ps", 2)

        units = []
        outs = []
        for c, width in enumerate(CHUNKS):
            col0 = sum(CHUNKS[:c])
            count = BANK // width
            units.extend((col0, width, g, t0, count) for g in range(GROUPS) for t0 in range(0, PACK, count))
            outs.extend((col0, width, j0) for j0 in range(0, M // P, count))
        last = len(units) - 1

        x_rows = x.rearrange("(g p t) k -> g p t k", p=P, t=PACK)
        lat_rows = lat.rearrange("(g p t) q -> g p t q", p=P, t=PACK)
        y_rows = y.rearrange("(g p t) q -> g p t q", p=P, t=PACK)
        v_rows = v_bytes.rearrange("(g p t) m -> g p t m", p=P, t=PACK)
        gam_flat = gam_words[0].rearrange("p n t -> p (n t)")

        def load_pair(dst, rows, j, width):
            nc.sync.dma_start(out=dst[j][:], in_=rows[j // 2][:, 2 * (j % 2) : 2 * (j % 2) + 2, :width])

        def load_b(arm, part):
            rows = b[arm].rearrange("(p t) q -> p t q", t=PACK)
            nc.sync.dma_start(out=b_raw[arm * PARTS + part][:], in_=rows[:, :, part * PART : (part + 1) * PART])

        def load_scores_first(j):
            load_pair(lat_first, lat_rows, j, PART)
            load_pair(y_first, y_rows, j, PART)

        def load_scores_rest(g):
            nc.sync.dma_start(out=lat_rest[g][:], in_=lat_rows[g][:, :, PART:])
            nc.sync.dma_start(out=y_rest[g][:], in_=y_rows[g][:, :, PART:])

        nc.vector.memset(gam_plane[:].bitcast(I32), 0)
        nc.vector.memset(zero[:], 0.0)
        make_identity(nc, ident[:])
        make_identity(nc, ident_bf[:])

        nc.sync.dma_start(out=v_fac[:], in_=v_scale.rearrange("(g p t) o -> p g (t o)", p=P, t=PACK))
        load_pair(v_raw, v_rows, 0, M)
        load_pair(x_raw, x_rows, 0, KX)
        load_b(1, 0)
        for quad in range(4):
            nc.scalar.dma_start(
                out=gam_plane[32 * quad : 32 * quad + 4, :].bitcast(I32),
                in_=gam_scales[0, 4 * quad : 4 * quad + 4, :].bitcast(I32),
            )
        nc.scalar.activation(out=one[:], in_=zero[:], func=ACT.Exp)
        nc.sync.dma_start(out=gam_first[:].bitcast(I32), in_=gam_flat[:, : PART * PACK].bitcast(I32))
        load_pair(v_raw, v_rows, 1, M)
        load_pair(x_raw, x_rows, 1, KX)
        load_b(0, 0)
        load_scores_first(0)
        nc.sync.dma_start(out=w_raw[:], in_=w.rearrange("(g p t) -> p g t", p=P, t=PACK))
        load_pair(x_raw, x_rows, 2, KX)
        load_scores_first(1)
        load_pair(x_raw, x_rows, 3, KX)
        load_b(1, 1)
        load_scores_first(2)
        load_b(0, 1)
        load_scores_first(3)
        nc.sync.dma_start(out=gam_rest[:].bitcast(I32), in_=gam_flat[:, PART * PACK :].bitcast(I32))
        load_pair(v_raw, v_rows, 2, M)
        load_pair(v_raw, v_rows, 3, M)
        for g in range(GROUPS):
            load_scores_rest(g)
            load_b(1, 2 + g)
            load_b(0, 2 + g)

        def quantize(codes, scales, src):
            nc.vector.quantize_mx(out=codes.bitcast(FP8X4), scales=scales, in_=src)

        def interleave(on_vector, dst, src, negate):
            dst_v = dst.rearrange("p (c i t) -> p c t i", i=RUN, t=PACK)
            src_v = src.rearrange("p t (c i) -> p c t i", i=RUN)
            if on_vector and negate:
                nc.vector.tensor_scalar(out=dst_v, in0=src_v, scalar1=-1.0, scalar2=None, op0=ALU.mult)
            elif on_vector:
                nc.vector.tensor_copy(out=dst_v, in_=src_v)
            elif negate:
                nc.scalar.activation(out=dst_v, in_=src_v, func=ACT.Copy, scale=-1.0)
            else:
                nc.scalar.copy(out=dst_v, in_=src_v)

        turned = []

        def turn(src):
            bank = out_ps[len(turned) % 2][:].bitcast(BF16)
            turned.append(bank)
            for h in range(PART // P):
                nc.tensor.matmul(out=bank[:, h * BANK : (h + 1) * BANK].rearrange("p (c t) -> p c t", t=PACK), lhsT=ident_bf[:],
                                 rhs=src[:, :, h * P : (h + 1) * P].rearrange("p t c -> p c t"), start=True, stop=True)
            return bank

        def x_turn(j):
            words = x_raw[j][:].rearrange("p a k -> p (a k)").bitcast(F32)
            half = KX // 2
            for a in range(2):
                for u in range(2):
                    nc.tensor.transpose(out_ps[j % 2][:, (2 * a + u) * P : (2 * a + u + 1) * P], words[:, a * half + u : (a + 1) * half : 2], ident[:])

        def x_copy(j):
            nc.scalar.copy(
                out=x_woven[j % 2][:].bitcast(F32).rearrange("p (a r u) -> p a r u", a=2, u=2),
                in_=out_ps[j % 2][:].rearrange("p (a u r) -> p a r u", a=2, u=2),
            )

        def x_quant(j):
            quantize(x_codes[j][:], x_scales[j][:], x_woven[j % 2][:])

        def x_operand(g, t):
            cols = slice((t % 2) * P, (t % 2 + 1) * P)
            return x_codes[2 * g + t // 2][:, cols].bitcast(FP8X4), x_scales[2 * g + t // 2][:, cols]

        def b_operand(arm, col0, width):
            cols = slice(col0 % PART, col0 % PART + width)
            return b_codes[arm * PARTS + col0 // PART][:, cols].bitcast(FP8X4), b_scales[arm * PARTS + col0 // PART][:, cols]

        def gam_operand(col0, width):
            codes = gam_first[:, col0 : col0 + width] if col0 < PART else gam_rest[:, col0 - PART : col0 - PART + width]
            return codes.bitcast(FP8X4), gam_plane[:, col0 : col0 + width]

        def rows_times(bank, s, movers):
            col0, width, g, t0, count = units[s]
            for i in range(count):
                lhs, lhs_scale = x_operand(g, t0 + i)
                for n, (rhs, rhs_scale) in enumerate(movers):
                    nc.tensor.matmul_mx(out=bank[:, i * width : (i + 1) * width], lhsT=lhs, lhsT_scale=lhs_scale, rhs=rhs, rhs_scale=rhs_scale,
                                        start=(n == 0), stop=(n == len(movers) - 1))

        def mm_z(s):
            rows_times(z_ps[s % 2], s, [gam_operand(units[s][0], units[s][1])])

        def mm_diff(s):
            rows_times(diff_ps, s, [b_operand(1, units[s][0], units[s][1]), b_operand(0, units[s][0], units[s][1])])

        def mm_mu(s):
            col0, width, g, t0, count = units[s]
            for i in range(2):
                block, t = divmod(2 * i, count)
                lhs, lhs_scale = b_operand(1, col0 + block * P, P)
                pair = 2 * g + (t0 + t) // 2
                nc.tensor.matmul_mx(out=mu_ps[:, i * 2 * P : (i + 1) * 2 * P], lhsT=lhs, lhsT_scale=lhs_scale,
                                    rhs=x_codes[pair][:].bitcast(FP8X4), rhs_scale=x_scales[pair][:], start=True, stop=True)

        def mu_out(s):
            nc.scalar.activation(out=mu_neg[s % 2][:], in_=mu_ps[:], func=ACT.Copy, scale=-1.0)

        def rows_of(first, rest, s):
            col0, width, g, t0, count = units[s]
            if col0 < PART:
                return first[2 * g + t0 // 2][:]
            return rest[g][:, t0 : t0 + count, col0 - PART : col0 - PART + width]

        def by_t(flat, s):
            return flat.rearrange("p (t c) -> p t c", t=units[s][4])

        def mm_resid(s):
            col0, width, g, t0, count = units[s]
            bank = resid_ps[s % 2]
            nc.tensor.matmul(out=by_t(bank[:], s), lhsT=ident_bf[:], rhs=rows_of(y_first, y_rest, s), start=True, stop=False)
            for i in range(BANK // P):
                block, t = divmod(i, count)
                at = t * width + block * P
                nc.tensor.matmul(out=bank[:, at : at + P], lhsT=mu_neg[s % 2][:, i * P : (i + 1) * P], rhs=ident[:],
                                 is_transpose=True, start=False, stop=(i == BANK // P - 1))

        def exps(s):
            nc.scalar.activation(out=exp_neg[s % EXP_DEPTH][:], in_=z_ps[s % 2][:], func=ACT.Exp, scale=-1.0)
            nc.scalar.activation(out=exp_pos[s % EXP_DEPTH][:], in_=z_ps[s % 2][:], func=ACT.Exp, bias=ln_trim[:])

        def op_cap(s):
            nc.vector.tensor_scalar(out=by_t(cap[s % MID_DEPTH][:], s), in0=rows_of(lat_first, lat_rest, s), scalar1=0.0, scalar2=TRIM,
                                    op0=ALU.is_le, op1=ALU.subtract)

        def op_clip(s):
            f = exp_neg[s % EXP_DEPTH]
            nc.vector.tensor_scalar(out=f[:], in0=f[:], scalar1=ODDS_LO, scalar2=ODDS_HI, op0=ALU.max, op1=ALU.min)

        def spans(s):
            return [slice(0, BANK // 2), slice(BANK // 2, BANK)] if s == last else [slice(0, BANK)]

        def op_weigh(s):
            for cols in spans(s):
                nc.vector.scalar_tensor_tensor(out=acc[s % MID_DEPTH][:, cols], in0=exp_neg[s % EXP_DEPTH][:, cols], scalar=1.0,
                                               in1=resid_ps[s % 2][:, cols], op0=ALU.add, op1=ALU.mult)

        def op_contrast(s):
            for cols in spans(s):
                nc.vector.tensor_tensor(out=acc[s % MID_DEPTH][:, cols], in0=acc[s % MID_DEPTH][:, cols], in1=diff_ps[:, cols], op=ALU.add)

        def op_arm(s):
            e = exp_pos[s % EXP_DEPTH]
            nc.vector.scalar_tensor_tensor(out=e[:], in0=e[:], scalar=TRIM * ODDS_LO, in1=cap[s % MID_DEPTH][:], op0=ALU.max, op1=ALU.min)

        def closes_block(s):
            return units[s][3] + units[s][4] == PACK

        def block_slot(s):
            return len([r for r in range(s) if closes_block(r)]) % 2

        def op_score(s):
            col0, width, g, t0, count = units[s]
            for i in range(count):
                cols = slice(i * width, (i + 1) * width)
                row = g * PACK + t0 + i
                nc.vector.scalar_tensor_tensor(out=g_rows[block_slot(s)][:, t0 + i, :width], in0=acc[s % MID_DEPTH][:, cols],
                                               scalar=w_fac[:, row : row + 1], in1=exp_pos[s % EXP_DEPTH][:, cols], op0=ALU.mult, op1=ALU.mult)

        def g_weave(s, on_vector):
            width = units[s][1]
            interleave(on_vector, g_woven[block_slot(s)][:, : width * PACK], g_rows[block_slot(s)][:, :, :width], False)

        g_done = []
        v_done = []
        weaves = []

        def g_quant(s):
            col0, width, g, t0, count = units[s]
            quantize(g_codes[g][:, col0 : col0 + width], g_scales[g][:, col0 : col0 + width], g_woven[block_slot(s)][:, : width * PACK])
            g_done.append((col0, g))

        def b_weave(arm, part, on_vector, bank=None):
            buf = woven[len(weaves) % WEAVE_DEPTH]
            weaves.append(buf)
            if bank is None:
                interleave(on_vector, buf[:], b_raw[arm * PARTS + part][:], arm == 0)
            else:
                nc.scalar.copy(out=buf[:], in_=bank)
            return lambda: quantize(b_codes[arm * PARTS + part][:], b_scales[arm * PARTS + part][:], buf[:])

        def v_widen(g, t, on_vector):
            src = v_raw[2 * g + t // 2][:, t % 2, :].bitcast(FP8)
            if on_vector:
                nc.vector.tensor_scalar(out=v_wide[g][:, t, :], in0=src, scalar1=v_fac[:, g, t : t + 1], scalar2=None, op0=ALU.mult)
            else:
                nc.scalar.activation(out=v_wide[g][:, t, :], in_=src, func=ACT.Copy, scale=v_fac[:, g, t : t + 1])

        def v_weave(g, part, on_vector, bank=None):
            buf = woven[len(weaves) % WEAVE_DEPTH]
            weaves.append(buf)
            cols = slice(part * PART, (part + 1) * PART)
            if bank is None:
                interleave(on_vector, buf[:], v_wide[g][:, :, cols], False)
            else:
                nc.scalar.copy(out=buf[:], in_=bank)

            def v_quant():
                quantize(v_codes[g][:, cols], v_scales[g][:, cols], buf[:])
                v_done.append((g, part))

            return v_quant

        def out_pass(dst, j, col0, width, g):
            rows = slice(j * P, (j + 1) * P)
            cols = slice(col0, col0 + width)
            nc.tensor.matmul_mx(out=dst, lhsT=v_codes[g][:, rows].bitcast(FP8X4), lhsT_scale=v_scales[g][:, rows],
                                rhs=g_codes[g][:, cols].bitcast(FP8X4), rhs_scale=g_scales[g][:, cols], start=(g == 0), stop=(g == GROUPS - 1))

        def out_scale(on_vector, dst, src):
            if on_vector:
                nc.vector.tensor_scalar(out=dst, in0=src, scalar1=1.0 / math.sqrt(N), scalar2=None, op0=ALU.mult)
            else:
                nc.scalar.activation(out=dst, in_=src, func=ACT.Copy, scale=1.0 / math.sqrt(N))

        def out_store(src, j0, count, col0, width):
            dst = out[j0 * P : (j0 + count) * P, col0 : col0 + width].rearrange("(j p) q -> p j q", p=P)
            nc.sync.dma_start(out=dst, in_=src.rearrange("p (j q) -> p j q", j=count))

        filled = []
        emptied = []
        looped = len(outs) - M // P * CHUNKS[-1] // BANK

        def fill_outs():
            while len(turned) == TURNS and len(filled) < min(len(emptied) + 2, looped):
                col0, width, j0 = outs[len(filled)]
                count = BANK // width
                parts = range(j0 * P // PART, ((j0 + count) * P - 1) // PART + 1)
                if not all((col0, g) in g_done and (g, part) in v_done for g in range(GROUPS) for part in parts):
                    break
                for i in range(count):
                    for g in range(GROUPS):
                        out_pass(out_ps[len(filled) % 2][:, i * width : (i + 1) * width], j0 + i, col0, width, g)
                filled.append(j0)

        def empty_outs(most):
            for n in range(most):
                if len(emptied) < len(filled):
                    k = len(emptied)
                    col0, width, j0 = outs[k]
                    out_scale(False, stage[k % STAGE_DEPTH][:], out_ps[k % 2][:])
                    out_store(stage[k % STAGE_DEPTH][:], j0, BANK // width, col0, width)
                    emptied.append(j0)
                    fill_outs()

        x_turn(0)
        v_widen(0, 0, False)
        v_widen(0, 1, True)
        nc.vector.tensor_scalar(out=ln_trim[:], in0=one[:], scalar1=math.log(TRIM), scalar2=None, op0=ALU.mult)
        x_copy(0)
        quant_b1 = b_weave(1, 0, True)
        v_widen(0, 2, False)
        quant_b1()
        x_quant(0)
        mm_mu(0)
        mm_z(0)
        x_turn(1)
        v_widen(0, 3, True)
        mu_out(0)
        exps(0)
        x_copy(1)
        quant_b0 = b_weave(0, 0, True)
        op_cap(0)
        quant_b0()
        op_clip(0)
        nc.vector.tensor_scalar(out=w_fac[:], in0=w_raw[:].rearrange("p g t -> p (g t)"), scalar1=-1.0 / TRIM, scalar2=None, op0=ALU.mult)
        mm_resid(0)
        mm_diff(0)
        x_turn(2)
        quant_v0 = v_weave(0, 0, True)
        x_quant(1)
        mm_mu(1)
        mm_z(1)
        quant_v1 = v_weave(0, 1, False)
        x_copy(2)
        mu_out(1)
        exps(1)
        x_turn(3)
        x_copy(3)
        op_arm(0)
        quant_v0()
        op_cap(1)
        quant_v2 = v_weave(0, 2, True)
        quant_v1()
        x_quant(2)
        mm_mu(2)
        mm_z(2)

        wide_steps = BANK // CHUNKS[0] * GROUPS
        due = [quant_v2, lambda: x_quant(3)]
        for s in range(len(units)):
            quants = due
            due = []
            room = SCALAR_ROOM
            late = s + 2 > last
            settled = s >= 2
            block_closed = s >= 1 and closes_block(s - 1)
            if block_closed and late:
                g_weave(s - 1, False)
            if s + 1 <= last:
                mm_resid(s + 1)
            b_parts = [part for part in range(1, PARTS) if s == max(0, wide_steps * part - 5)]
            v_parts = [(0, PARTS - 1)] if s == 1 else [(1, s - PACK + 1)] if PACK - 1 <= s < PACK - 1 + PARTS else []
            b_banks = [turn(b_raw[PARTS + part][:]) if part < PARTS - 1 else None for part in b_parts]
            v_banks = [turn(v_wide[g][:, :, part * PART : (part + 1) * PART]) for g, part in v_parts]
            if not late:
                mu_out(s + 2)
            if settled and s + 3 <= last:
                mm_mu(s + 3)
            if s + 1 <= last:
                op_clip(s + 1)
            op_weigh(s)
            if not late:
                exps(s + 2)
                room = room - 3
            if settled and s + 3 <= last:
                mm_z(s + 3)
            if s + 1 <= last:
                op_arm(s + 1)
            op_contrast(s)
            if block_closed:
                if not late and s != G_ON_VECTOR:
                    g_weave(s - 1, False)
                (quants if late else due).append(lambda r=s - 1: g_quant(r))
                if s != G_ON_VECTOR:
                    room = room - units[s - 1][1] * PACK // BANK
            for part, bank in zip(b_parts, b_banks):
                due.append(b_weave(1, part, False, bank))
                room = room - 2
            for (g, part), bank in zip(v_parts, v_banks):
                due.append(v_weave(g, part, False, bank))
            for part in range(1, PARTS):
                if s == wide_steps * part - 3:
                    due.append(b_weave(0, part, False))
                    room = room - 2
            v_rows_now = [t for t in range(PACK) if s == min(t, 2)]
            for t in v_rows_now:
                if t not in (1, 2):
                    v_widen(1, t, False)
            empty_outs(room)
            if s + 1 <= last:
                mm_diff(s + 1)
            if not late:
                op_cap(s + 2)
            if s == G_ON_VECTOR:
                g_weave(s - 1, True)
            op_score(s)
            for t in v_rows_now:
                if t in (1, 2):
                    v_widen(1, t, True)
            for run in quants:
                run()
            if not settled:
                mm_mu(s + 3)
                mm_z(s + 3)
            fill_outs()

        empty_outs(looped - len(emptied))
        col0, width = units[last][:2]
        spare = z_ps + [mu_ps] + resid_ps + [diff_ps] + out_ps
        for j in range(M // P):
            out_pass(spare[j][:, :width], j, col0, width, 0)
        g_weave(last, True)
        g_quant(last)
        for j in range(M // P):
            out_pass(spare[j][:, :width], j, col0, width, 1)
            both = stage[(looped + j // 2) % STAGE_DEPTH]
            out_scale(j % 2 == 1, both[:, (j % 2) * width : (j % 2 + 1) * width], spare[j][:, :width])
            if j % 2 == 1:
                out_store(both[:, : 2 * width], j - 1, 2, col0, width)
